import numpy as np
import ml_dtypes


def mxq(x, axis, fmt="e4m3"):
    dtype, down = {"e4m3": (ml_dtypes.float8_e4m3fn, 7), "e5m2": (ml_dtypes.float8_e5m2, 14)}[fmt]
    v = np.moveaxis(np.asarray(x, np.float32).astype(ml_dtypes.bfloat16).astype(np.float64), axis, -1)
    blocks = v.reshape(v.shape[:-1] + (-1, 32))
    amax = np.abs(blocks).max(-1, keepdims=True)
    byte = np.maximum(np.where(amax > 0, np.frexp(amax)[1] - 1 + 127, 0) - down, 1)
    scale = np.exp2(byte - 127.0)
    codes = (blocks / scale).astype(np.float32).astype(dtype).astype(np.float64)
    return np.moveaxis((codes * scale).reshape(v.shape), -1, axis)


WIDE = False


def mx_kscale(k):
    if not WIDE:
        return np.ones(k)
    levels = np.array([10, -10, 5, -5, 0])
    if k % 512:
        return np.exp2(np.random.permutation(np.resize(levels, k // 32))).repeat(32)
    a = np.empty((k // 512, 16))
    for p in range(k // 512):
        a[p, :8] = np.random.permutation(np.resize(levels, 8))
        for g in range(8):
            far = levels[np.abs(levels - a[p, g]) >= 10]
            a[p, g + 8] = far[np.random.randint(len(far))]
    return np.exp2(a.ravel()).repeat(32)


def f64(x):
    return np.asarray(x).astype(np.float64)


def striped(idx):
    return np.tile(idx.reshape(-1, 16).T, (8, 1)).astype(np.uint16)


def unstriped(offs):
    return offs[:16].T.reshape(-1).astype(np.int64)


E2M1 = np.array([0.0, 0.5, 1.0, 1.5, 2.0, 3.0, 4.0, 6.0, -0.0, -0.5, -1.0, -1.5, -2.0, -3.0, -4.0, -6.0])


def pack_weight(w, fmt):
    k, n = w.shape
    w = f64(np.asarray(w, np.float32).astype(ml_dtypes.bfloat16)).reshape(k // 32, 32, n)
    amax = np.abs(w).max(1)
    if fmt == "e4m3":
        byte = np.frexp(amax)[1] - 1 + 127 - 7
    else:
        mant, ex = np.frexp(amax / 6.0)
        byte = np.where(mant > 0.5, ex, ex - 1) + 127
    byte = np.clip(np.where(amax > 0, byte, 1), 1, 254)
    scaled = (w * np.exp2(127.0 - byte)[:, None, :]).reshape(k, n).astype(np.float32)
    by_word = np.ascontiguousarray(scaled.reshape(k // 512, 128, 4, n).transpose(0, 1, 3, 2))
    if fmt == "e4m3":
        words = by_word.astype(ml_dtypes.float8_e4m3fn).view(np.uint8)
    else:
        c = by_word.astype(ml_dtypes.float4_e2m1fn).view(np.uint8) & 0xF
        words = (c[..., 0::2] | (c[..., 1::2] << 4)).reshape(k // 512, 128, 2 * n)
    return np.ascontiguousarray(words), np.ascontiguousarray(byte.astype(np.uint8).reshape(k // 512, 16, n))


def unpack_weight(words, scales, fmt):
    g, _, n = scales.shape
    words = np.ascontiguousarray(words).reshape(g, 128, n, -1)
    if fmt == "e4m3":
        vals = words.view(ml_dtypes.float8_e4m3fn).astype(np.float64)
    else:
        nib = np.empty((g, 128, n, 4), np.uint8)
        nib[..., 0::2] = words & 0xF
        nib[..., 1::2] = words >> 4
        vals = E2M1[nib]
    vals = vals * np.repeat(np.exp2(scales.astype(np.float64) - 127.0), 8, axis=1)[..., None]
    return vals.transpose(0, 1, 3, 2).reshape(g * 512, n)


def gelu(v):
    return 0.5 * v * (1.0 + np.tanh(np.sqrt(2.0 / np.pi) * (v + 0.044715 * v**3)))


K, T, E, C, H, N = 512, 512, 2, 256, 512, 128


def by_expert(wq, xq):
    return np.concatenate([wq[e].T @ xq[:, e * C:(e + 1) * C] for e in range(E)], axis=1)


def setup_inputs():
    n = np.random.standard_normal
    s = mx_kscale(K)
    u = mx_kscale(H)
    slot_token = np.random.permutation(T)[:E * C]
    partner = np.concatenate([np.random.permutation(T) for _ in range(-(-E * C // T))])[:E * C]
    x = pack_weight(n((K, T)) * s[:, None], "e4m3")
    w1 = [pack_weight(m, "e2m1") for m in n((E, K, H)) / np.sqrt(K) / s[None, :, None] * u]
    wp = [pack_weight(m, "e2m1") for m in n((E, K, H)) / np.sqrt(K) / s[None, :, None] * u]
    w2 = [pack_weight(m, "e2m1") for m in n((E, H, N)) / np.sqrt(H) / u[None, :, None]]
    return {
        "x_words": x[0],
        "x_scales": x[1],
        "w1_words": np.stack([m[0] for m in w1]),
        "w1_scales": np.stack([m[1] for m in w1]),
        "wp_words": np.stack([m[0] for m in wp]),
        "wp_scales": np.stack([m[1] for m in wp]),
        "w2_words": np.stack([m[0] for m in w2]),
        "w2_scales": np.stack([m[1] for m in w2]),
        "gate": np.tile(np.random.uniform(0.2, 1.0, E * C), (128, 1)).astype(np.float32),
        "offs": striped(slot_token),
        "offs2": striped(partner),
    }


def reference(x_words, x_scales, w1_words, w1_scales, wp_words, wp_scales, w2_words, w2_scales, gate, offs, offs2):
    w1 = np.stack([unpack_weight(w1_words[e], w1_scales[e], "e2m1") for e in range(E)])
    wp = np.stack([unpack_weight(wp_words[e], wp_scales[e], "e2m1") for e in range(E)])
    w2 = np.stack([unpack_weight(w2_words[e], w2_scales[e], "e2m1") for e in range(E)])
    idx, idx2 = unstriped(offs), unstriped(offs2)
    x = unpack_weight(x_words, x_scales, "e4m3")
    h = gelu(by_expert(w1, x[:, idx]) + by_expert(wp, x[:, idx2]))
    y = by_expert(w2, mxq(h, 0, "e4m3"))
    out = np.zeros((N, T))
    out[:, idx] = f64(gate[:1]) * y
    return out

@@ -1,0 +1,106 @@
+from contextlib import ExitStack
+
+import concourse.mybir as mybir
+from concourse.masks import make_identity
+
+K, T, E, C, H, N = 512, 512, 2, 256, 512, 128
+FLOPS = 2 * E * C * (2 * K * H + H * N)
+
+F32 = mybir.dt.float32
+BF16 = mybir.dt.bfloat16
+I32 = mybir.dt.int32
+U32 = mybir.dt.uint32
+U16 = mybir.dt.uint16
+U8 = mybir.dt.uint8
+FP8X4 = mybir.dt.float8_e4m3fn_x4
+FP4X4 = mybir.dt.float4_e2m1fn_x4
+
+P = 128
+S = 128
+TILES = E * C // S
+LC = S // 16
+
+
+def load_plane(queue, plane, rows):
+    for q in range(4):
+        queue.dma_start(out=plane[32 * q:32 * q + 4, :, :], in_=rows[:, 4 * q:4 * q + 4, :].rearrange("e r n -> r e n"))
+
+
+def tile_moe_duo_gelu_kernel(tc, x_words, x_scales, w1_words, w1_scales, wp_words, wp_scales, w2_words, w2_scales, gate, offs, offs2, out):
+    nc = tc.nc
+    with ExitStack() as ctx:
+        keep = ctx.enter_context(tc.tile_pool(name="keep", bufs=1))
+        work = ctx.enter_context(tc.tile_pool(name="work", bufs=TILES))
+        pre_pool = ctx.enter_context(tc.psum_pool(name="pre", bufs=4))
+        tr_pool = ctx.enter_context(tc.psum_pool(name="tr", bufs=2))
+        y_pool = ctx.enter_context(tc.psum_pool(name="y", bufs=2))
+
+        xw = keep.tile([P, T], I32, name="xw", align_bytes=64)
+        xs = keep.tile([P, T], U8, name="xs", align_bytes=64)
+        lists = [keep.tile([P, E * C // 16], U16, name="list%d" % a) for a in range(2)]
+        ww = [keep.tile([P, E, 2 * H], U8, name="ww%d" % a, align_bytes=64) for a in range(2)]
+        ws = [keep.tile([P, E, H], U8, name="ws%d" % a, align_bytes=64) for a in range(2)]
+        w2w = keep.tile([P, E, 2 * N], U8, name="w2w", align_bytes=64)
+        w2s = keep.tile([P, E, N], U8, name="w2s", align_bytes=64)
+        g = keep.tile([P, E * C], F32, name="g")
+        res = keep.tile([P, T], F32, name="res")
+        ident = keep.tile([P, P], F32, name="ident")
+
+        nc.vector.memset(xs[:].bitcast(I32), 0)
+        for plane in (ws[0], ws[1], w2s):
+            nc.vector.memset(plane[:].bitcast(I32), 0)
+
+        nc.sync.dma_start(out=xw[:], in_=x_words[0].rearrange("p n t -> p (n t)").bitcast(I32))
+        nc.sync.dma_start(lists[0][:], offs)
+        nc.sync.dma_start(lists[1][:], offs2)
+        load_plane(nc.scalar, xs[:].bitcast(I32).unsqueeze(1), x_scales.bitcast(I32))
+        for a, words in enumerate((w1_words, wp_words)):
+            nc.gpsimd.dma_start(out=ww[a][:].bitcast(I32), in_=words.rearrange("e s p n -> p (e s) n").bitcast(I32))
+        for a, scales in enumerate((w1_scales, wp_scales)):
+            load_plane(nc.sync, ws[a][:].bitcast(I32), scales.rearrange("e s r n -> (e s) r n").bitcast(I32))
+        load_plane(nc.sync, w2s[:].bitcast(I32), w2_scales.rearrange("e s r n -> (e s) r n").bitcast(I32))
+        nc.sync.dma_start(out=w2w[:].bitcast(I32), in_=w2_words.rearrange("e s p n -> p (e s) n").bitcast(I32))
+        nc.sync.dma_start(out=g[:], in_=gate)
+        make_identity(nc, ident[:])
+
+        pres = []
+        for c in range(TILES):
+            e = c * S // C
+            pre = pre_pool.tile([P, H], F32, name="pre")
+            for a in range(2):
+                sel = lists[a][:, c * LC:(c + 1) * LC]
+                gw = work.tile([P, S], U32, name="gw%d" % a, align_bytes=64)
+                gs = work.tile([P, S], U8, name="gs%d" % a, align_bytes=64)
+                nc.vector.tensor_copy(gw[:], xw[:].bitcast(U32).indirect(sel))
+                nc.vector.tensor_copy(gs[:], xs[:].indirect(sel))
+                nc.tensor.matmul_mx(out=pre[:], lhsT=gw[:].bitcast(FP8X4), lhsT_scale=gs[:],
+                                    rhs=ww[a][:, e, :].bitcast(FP4X4), rhs_scale=ws[a][:, e, :],
+                                    start=(a == 0), stop=(a == 1))
+            pres.append(pre)
+
+        hts = []
+        for c in range(TILES):
+            h = work.tile([P, H], BF16, name="h", align_bytes=64)
+            nc.scalar.activation(h[:].rearrange("p (u m d) -> p u m d", u=2, d=2),
+                                 pres[c][:].rearrange("p (m u d) -> p u m d", u=2, d=2),
+                                 mybir.ActivationFunctionType.Gelu_apprx_tanh)
+            tr = tr_pool.tile([P, 2, S], F32, name="tr")
+            for u in range(2):
+                nc.tensor.transpose(tr[:, u, :], h[:].bitcast(F32)[:, u * P:(u + 1) * P], ident[:])
+            ht = work.tile([P, 4 * S], BF16, name="ht", align_bytes=64)
+            nc.scalar.copy(ht[:].bitcast(F32).rearrange("p (j u) -> p j u", u=2), tr[:].rearrange("p u j -> p j u"))
+            hts.append(ht)
+
+        for c in range(TILES):
+            e = c * S // C
+            hq = work.tile([P, S], U32, name="hq", align_bytes=64)
+            hs = work.tile([P, S], U8, name="hs", align_bytes=64)
+            nc.vector.quantize_mx(out=hq[:].bitcast(FP8X4), scales=hs[:], in_=hts[c][:])
+            y = y_pool.tile([P, S], F32, name="y")
+            nc.tensor.matmul_mx(out=y[:], lhsT=w2w[:, e, :].bitcast(FP4X4), lhsT_scale=w2s[:, e, :],
+                                rhs=hq[:].bitcast(FP8X4), rhs_scale=hs[:], start=True, stop=True)
+            yg = work.tile([P, S], F32, name="yg")
+            nc.vector.tensor_tensor(yg[:], y[:], g[:, c * S:(c + 1) * S], mybir.AluOpType.mult)
+            nc.vector.tensor_copy(res[:].indirect(lists[0][:, c * LC:(c + 1) * LC]), yg[:])
+
+        nc.sync.dma_start(out=out, in_=res[:])

@@ -19,6 +19,7 @@ P = 128
 S = 128
 TILES = E * C // S
 LC = S // 16
+PIECES = ((0, 2), (2, 3), (3, 4))
 
 
 def load_plane(queue, plane, rows):
@@ -54,53 +55,52 @@ def tile_moe_duo_gelu_kernel(tc, x_words, x_scales, w1_words, w1_scales, wp_word
         nc.sync.dma_start(lists[0][:], offs)
         nc.sync.dma_start(lists[1][:], offs2)
         load_plane(nc.scalar, xs[:].bitcast(I32).unsqueeze(1), x_scales.bitcast(I32))
-        for a, words in enumerate((w1_words, wp_words)):
-            nc.gpsimd.dma_start(out=ww[a][:].bitcast(I32), in_=words.rearrange("e s p n -> p (e s) n").bitcast(I32))
-        for a, scales in enumerate((w1_scales, wp_scales)):
+        for a, (queue, words) in enumerate(((nc.sync, w1_words), (nc.gpsimd, wp_words))):
+            queue.dma_start(out=ww[a][:].bitcast(I32), in_=words.rearrange("e s p n -> p (e s) n").bitcast(I32))
+        make_identity(nc, ident[:])
+        for a, scales in ((1, wp_scales), (0, w1_scales)):
             load_plane(nc.sync, ws[a][:].bitcast(I32), scales.rearrange("e s r n -> (e s) r n").bitcast(I32))
         load_plane(nc.sync, w2s[:].bitcast(I32), w2_scales.rearrange("e s r n -> (e s) r n").bitcast(I32))
-        nc.sync.dma_start(out=w2w[:].bitcast(I32), in_=w2_words.rearrange("e s p n -> p (e s) n").bitcast(I32))
-        nc.sync.dma_start(out=g[:], in_=gate)
-        make_identity(nc, ident[:])
+        nc.gpsimd.dma_start(out=w2w[:].bitcast(I32), in_=w2_words.rearrange("e s p n -> p (e s) n").bitcast(I32))
+        nc.gpsimd.dma_start(out=g[:], in_=gate)
 
-        pres = []
+        gathered = {}
+        for c0, c1 in PIECES:
+            for a in range(2):
+                sel = lists[a][:, c0 * LC:c1 * LC]
+                gw = keep.tile([P, (c1 - c0) * S], U32, name="gw%d_%d" % (a, c0), align_bytes=64)
+                gs = keep.tile([P, (c1 - c0) * S], U8, name="gs%d_%d" % (a, c0), align_bytes=64)
+                nc.vector.tensor_copy(gw[:], xw[:].bitcast(U32).indirect(sel))
+                nc.vector.tensor_copy(gs[:], xs[:].indirect(sel))
+                for c in range(c0, c1):
+                    cols = slice((c - c0) * S, (c - c0 + 1) * S)
+                    gathered[c, a] = (gw[:, cols], gs[:, cols])
+
         for c in range(TILES):
             e = c * S // C
             pre = pre_pool.tile([P, H], F32, name="pre")
             for a in range(2):
-                sel = lists[a][:, c * LC:(c + 1) * LC]
-                gw = work.tile([P, S], U32, name="gw%d" % a, align_bytes=64)
-                gs = work.tile([P, S], U8, name="gs%d" % a, align_bytes=64)
-                nc.vector.tensor_copy(gw[:], xw[:].bitcast(U32).indirect(sel))
-                nc.vector.tensor_copy(gs[:], xs[:].indirect(sel))
-                nc.tensor.matmul_mx(out=pre[:], lhsT=gw[:].bitcast(FP8X4), lhsT_scale=gs[:],
+                gw, gs = gathered[c, a]
+                nc.tensor.matmul_mx(out=pre[:], lhsT=gw.bitcast(FP8X4), lhsT_scale=gs,
                                     rhs=ww[a][:, e, :].bitcast(FP4X4), rhs_scale=ws[a][:, e, :],
                                     start=(a == 0), stop=(a == 1))
-            pres.append(pre)
-
-        hts = []
-        for c in range(TILES):
             h = work.tile([P, H], BF16, name="h", align_bytes=64)
             nc.scalar.activation(h[:].rearrange("p (u m d) -> p u m d", u=2, d=2),
-                                 pres[c][:].rearrange("p (m u d) -> p u m d", u=2, d=2),
+                                 pre[:].rearrange("p (m u d) -> p u m d", u=2, d=2),
                                  mybir.ActivationFunctionType.Gelu_apprx_tanh)
             tr = tr_pool.tile([P, 2, S], F32, name="tr")
             for u in range(2):
                 nc.tensor.transpose(tr[:, u, :], h[:].bitcast(F32)[:, u * P:(u + 1) * P], ident[:])
             ht = work.tile([P, 4 * S], BF16, name="ht", align_bytes=64)
             nc.scalar.copy(ht[:].bitcast(F32).rearrange("p (j u) -> p j u", u=2), tr[:].rearrange("p u j -> p j u"))
-            hts.append(ht)
-
-        for c in range(TILES):
-            e = c * S // C
             hq = work.tile([P, S], U32, name="hq", align_bytes=64)
             hs = work.tile([P, S], U8, name="hs", align_bytes=64)
-            nc.vector.quantize_mx(out=hq[:].bitcast(FP8X4), scales=hs[:], in_=hts[c][:])
+            nc.vector.quantize_mx(out=hq[:].bitcast(FP8X4), scales=hs[:], in_=ht[:])
             y = y_pool.tile([P, S], F32, name="y")
             nc.tensor.matmul_mx(out=y[:], lhsT=w2w[:, e, :].bitcast(FP4X4), lhsT_scale=w2s[:, e, :],
                                 rhs=hq[:].bitcast(FP8X4), rhs_scale=hs[:], start=True, stop=True)
             yg = work.tile([P, S], F32, name="yg")
-            nc.vector.tensor_tensor(yg[:], y[:], g[:, c * S:(c + 1) * S], mybir.AluOpType.mult)
-            nc.vector.tensor_copy(res[:].indirect(lists[0][:, c * LC:(c + 1) * LC]), yg[:])
+            nc.scalar.copy(yg[:], y[:])
+            nc.vector.tensor_tensor(res[:].indirect(lists[0][:, c * LC:(c + 1) * LC]), yg[:], g[:, c * S:(c + 1) * S], mybir.AluOpType.mult)
 
         nc.sync.dma_start(out=out, in_=res[:])

@@ -19,6 +19,7 @@ P = 128
 S = 128
 TILES = E * C // S
 LC = S // 16
+SCATTERS = ((0, 1), (1, 3), (3, 4))
 PIECES = ((0, 2), (2, 3), (3, 4))
 
 
@@ -32,9 +33,9 @@ def tile_moe_duo_gelu_kernel(tc, x_words, x_scales, w1_words, w1_scales, wp_word
     with ExitStack() as ctx:
         keep = ctx.enter_context(tc.tile_pool(name="keep", bufs=1))
         work = ctx.enter_context(tc.tile_pool(name="work", bufs=TILES))
-        pre_pool = ctx.enter_context(tc.psum_pool(name="pre", bufs=4))
+        pre_pool = ctx.enter_context(tc.psum_pool(name="pre", bufs=3))
         tr_pool = ctx.enter_context(tc.psum_pool(name="tr", bufs=2))
-        y_pool = ctx.enter_context(tc.psum_pool(name="y", bufs=2))
+        y_pool = ctx.enter_context(tc.psum_pool(name="y", bufs=3))
 
         xw = keep.tile([P, T], I32, name="xw", align_bytes=64)
         xs = keep.tile([P, T], U8, name="xs", align_bytes=64)
@@ -47,22 +48,26 @@ def tile_moe_duo_gelu_kernel(tc, x_words, x_scales, w1_words, w1_scales, wp_word
         res = keep.tile([P, T], F32, name="res")
         ident = keep.tile([P, P], F32, name="ident")
 
-        nc.vector.memset(xs[:].bitcast(I32), 0)
         for plane in (ws[0], ws[1], w2s):
             nc.vector.memset(plane[:].bitcast(I32), 0)
 
-        nc.sync.dma_start(out=xw[:], in_=x_words[0].rearrange("p n t -> p (n t)").bitcast(I32))
+        def load_token_scales(queue, q):
+            rows = x_scales[0, 4 * q:4 * q + 4, :].bitcast(I32)
+            queue.dma_start(out=xs[32 * q:32 * q + 32, :].bitcast(I32), in_=rows.unsqueeze(0).broadcast_to([8, 4, T // 4]))
+
         nc.sync.dma_start(lists[0][:], offs)
+        for q in range(4):
+            load_token_scales(nc.scalar, q)
+        nc.sync.dma_start(out=xw[:], in_=x_words[0].rearrange("p n t -> p (n t)").bitcast(I32))
         nc.sync.dma_start(lists[1][:], offs2)
-        load_plane(nc.scalar, xs[:].bitcast(I32).unsqueeze(1), x_scales.bitcast(I32))
+        make_identity(nc, ident[:])
         for a, (queue, words) in enumerate(((nc.sync, w1_words), (nc.gpsimd, wp_words))):
             queue.dma_start(out=ww[a][:].bitcast(I32), in_=words.rearrange("e s p n -> p (e s) n").bitcast(I32))
-        make_identity(nc, ident[:])
-        for a, scales in ((1, wp_scales), (0, w1_scales)):
-            load_plane(nc.sync, ws[a][:].bitcast(I32), scales.rearrange("e s r n -> (e s) r n").bitcast(I32))
+        for a, queue, scales in ((1, nc.scalar, wp_scales), (0, nc.sync, w1_scales)):
+            load_plane(queue, ws[a][:].bitcast(I32), scales.rearrange("e s r n -> (e s) r n").bitcast(I32))
         load_plane(nc.sync, w2s[:].bitcast(I32), w2_scales.rearrange("e s r n -> (e s) r n").bitcast(I32))
-        nc.gpsimd.dma_start(out=w2w[:].bitcast(I32), in_=w2_words.rearrange("e s p n -> p (e s) n").bitcast(I32))
-        nc.gpsimd.dma_start(out=g[:], in_=gate)
+        nc.sync.dma_start(out=w2w[:].bitcast(I32), in_=w2_words.rearrange("e s p n -> p (e s) n").bitcast(I32))
+        nc.sync.dma_start(out=g[:], in_=gate)
 
         gathered = {}
         for c0, c1 in PIECES:
@@ -76,7 +81,10 @@ def tile_moe_duo_gelu_kernel(tc, x_words, x_scales, w1_words, w1_scales, wp_word
                     cols = slice((c - c0) * S, (c - c0 + 1) * S)
                     gathered[c, a] = (gw[:, cols], gs[:, cols])
 
-        for c in range(TILES):
+        hts, ys = {}, {}
+        yall = keep.tile([P, E * C], F32, name="yall")
+
+        def front(c):
             e = c * S // C
             pre = pre_pool.tile([P, H], F32, name="pre")
             for a in range(2):
@@ -92,15 +100,32 @@ def tile_moe_duo_gelu_kernel(tc, x_words, x_scales, w1_words, w1_scales, wp_word
             for u in range(2):
                 nc.tensor.transpose(tr[:, u, :], h[:].bitcast(F32)[:, u * P:(u + 1) * P], ident[:])
             ht = work.tile([P, 4 * S], BF16, name="ht", align_bytes=64)
-            nc.scalar.copy(ht[:].bitcast(F32).rearrange("p (j u) -> p j u", u=2), tr[:].rearrange("p u j -> p j u"))
+            (nc.vector.tensor_copy if c in (0, 1) else nc.scalar.copy)(ht[:].bitcast(F32).rearrange("p (j u) -> p j u", u=2), tr[:].rearrange("p u j -> p j u"))
+            hts[c] = ht
+
+        def second(c):
+            e = c * S // C
             hq = work.tile([P, S], U32, name="hq", align_bytes=64)
             hs = work.tile([P, S], U8, name="hs", align_bytes=64)
-            nc.vector.quantize_mx(out=hq[:].bitcast(FP8X4), scales=hs[:], in_=ht[:])
+            nc.vector.quantize_mx(out=hq[:].bitcast(FP8X4), scales=hs[:], in_=hts[c][:])
             y = y_pool.tile([P, S], F32, name="y")
             nc.tensor.matmul_mx(out=y[:], lhsT=w2w[:, e, :].bitcast(FP4X4), lhsT_scale=w2s[:, e, :],
                                 rhs=hq[:].bitcast(FP8X4), rhs_scale=hs[:], start=True, stop=True)
-            yg = work.tile([P, S], F32, name="yg")
-            nc.scalar.copy(yg[:], y[:])
-            nc.vector.tensor_tensor(res[:].indirect(lists[0][:, c * LC:(c + 1) * LC]), yg[:], g[:, c * S:(c + 1) * S], mybir.AluOpType.mult)
+            ys[c] = y
+
+        def empty(c):
+            nc.scalar.copy(yall[:, c * S:(c + 1) * S], ys[c][:])
+
+        def scatter(c):
+            for c0, c1 in SCATTERS:
+                if c1 - 1 == c:
+                    cols = slice(c0 * S, c1 * S)
+                    nc.vector.tensor_tensor(res[:].indirect(lists[0][:, c0 * LC:c1 * LC]), yall[:, cols], g[:, cols], mybir.AluOpType.mult)
+
+        stages = ((front, 0), (second, 1), (empty, 2), (scatter, 3))
+        for step in range(TILES + 3):
+            for stage, lag in stages:
+                if 0 <= step - lag < TILES:
+                    stage(step - lag)
 
         nc.sync.dma_start(out=out, in_=res[:])

@@ -19,8 +19,7 @@ P = 128
 S = 128
 TILES = E * C // S
 LC = S // 16
-SCATTERS = ((0, 1), (1, 3), (3, 4))
-PIECES = ((0, 2), (2, 3), (3, 4))
+PIECES = ((0, 1), (1, 2), (2, 4))
 
 
 def load_plane(queue, plane, rows):
@@ -33,9 +32,10 @@ def tile_moe_duo_gelu_kernel(tc, x_words, x_scales, w1_words, w1_scales, wp_word
     with ExitStack() as ctx:
         keep = ctx.enter_context(tc.tile_pool(name="keep", bufs=1))
         work = ctx.enter_context(tc.tile_pool(name="work", bufs=TILES))
-        pre_pool = ctx.enter_context(tc.psum_pool(name="pre", bufs=3))
+        ring = ctx.enter_context(tc.tile_pool(name="ring", bufs=2))
+        pre_pool = ctx.enter_context(tc.psum_pool(name="pre", bufs=2))
         tr_pool = ctx.enter_context(tc.psum_pool(name="tr", bufs=2))
-        y_pool = ctx.enter_context(tc.psum_pool(name="y", bufs=3))
+        y_pool = ctx.enter_context(tc.psum_pool(name="y", bufs=4))
 
         xw = keep.tile([P, T], I32, name="xw", align_bytes=64)
         xs = keep.tile([P, T], U8, name="xs", align_bytes=64)
@@ -56,33 +56,36 @@ def tile_moe_duo_gelu_kernel(tc, x_words, x_scales, w1_words, w1_scales, wp_word
             queue.dma_start(out=xs[32 * q:32 * q + 32, :].bitcast(I32), in_=rows.unsqueeze(0).broadcast_to([8, 4, T // 4]))
 
         nc.sync.dma_start(lists[0][:], offs)
-        for q in range(4):
-            load_token_scales(nc.scalar, q)
-        nc.sync.dma_start(out=xw[:], in_=x_words[0].rearrange("p n t -> p (n t)").bitcast(I32))
         nc.sync.dma_start(lists[1][:], offs2)
+        for q in range(4):
+            load_token_scales(nc.scalar if q else nc.sync, q)
+        nc.scalar.dma_start(out=xw[:], in_=x_words[0].rearrange("p n t -> p (n t)").bitcast(I32))
         make_identity(nc, ident[:])
         for a, (queue, words) in enumerate(((nc.sync, w1_words), (nc.gpsimd, wp_words))):
             queue.dma_start(out=ww[a][:].bitcast(I32), in_=words.rearrange("e s p n -> p (e s) n").bitcast(I32))
-        for a, queue, scales in ((1, nc.scalar, wp_scales), (0, nc.sync, w1_scales)):
+        for a, queue, scales in ((0, nc.scalar, w1_scales), (1, nc.sync, wp_scales)):
             load_plane(queue, ws[a][:].bitcast(I32), scales.rearrange("e s r n -> (e s) r n").bitcast(I32))
         load_plane(nc.sync, w2s[:].bitcast(I32), w2_scales.rearrange("e s r n -> (e s) r n").bitcast(I32))
         nc.sync.dma_start(out=w2w[:].bitcast(I32), in_=w2_words.rearrange("e s p n -> p (e s) n").bitcast(I32))
         nc.sync.dma_start(out=g[:], in_=gate)
 
         gathered = {}
-        for c0, c1 in PIECES:
-            for a in range(2):
-                sel = lists[a][:, c0 * LC:c1 * LC]
-                gw = keep.tile([P, (c1 - c0) * S], U32, name="gw%d_%d" % (a, c0), align_bytes=64)
-                gs = keep.tile([P, (c1 - c0) * S], U8, name="gs%d_%d" % (a, c0), align_bytes=64)
-                nc.vector.tensor_copy(gw[:], xw[:].bitcast(U32).indirect(sel))
-                nc.vector.tensor_copy(gs[:], xs[:].indirect(sel))
-                for c in range(c0, c1):
-                    cols = slice((c - c0) * S, (c - c0 + 1) * S)
-                    gathered[c, a] = (gw[:, cols], gs[:, cols])
+
+        def gather(c):
+            for c0, c1 in PIECES:
+                if c0 == c:
+                    for a in range(2):
+                        sel = lists[a][:, c0 * LC:c1 * LC]
+                        gw = keep.tile([P, (c1 - c0) * S], U32, name="gw%d_%d" % (a, c0), align_bytes=64)
+                        gs = ring.tile([P, (c1 - c0) * S], U8, name="gs%d" % a, align_bytes=64)
+                        nc.vector.tensor_copy(gs[:], xs[:].indirect(sel))
+                        nc.vector.tensor_copy(gw[:], xw[:].bitcast(U32).indirect(sel))
+                        for t in range(c0, c1):
+                            cols = slice((t - c0) * S, (t - c0 + 1) * S)
+                            gathered[t, a] = (gw[:, cols], gs[:, cols])
 
         hts, ys = {}, {}
-        yall = keep.tile([P, E * C], F32, name="yall")
+        rows = {}
 
         def front(c):
             e = c * S // C
@@ -92,7 +95,7 @@ def tile_moe_duo_gelu_kernel(tc, x_words, x_scales, w1_words, w1_scales, wp_word
                 nc.tensor.matmul_mx(out=pre[:], lhsT=gw.bitcast(FP8X4), lhsT_scale=gs,
                                     rhs=ww[a][:, e, :].bitcast(FP4X4), rhs_scale=ws[a][:, e, :],
                                     start=(a == 0), stop=(a == 1))
-            h = work.tile([P, H], BF16, name="h", align_bytes=64)
+            h = keep.tile([P, H], BF16, name="h%d" % c, tag="h%d" % c, align_bytes=64)
             nc.scalar.activation(h[:].rearrange("p (u m d) -> p u m d", u=2, d=2),
                                  pre[:].rearrange("p (m u d) -> p u m d", u=2, d=2),
                                  mybir.ActivationFunctionType.Gelu_apprx_tanh)
@@ -100,7 +103,7 @@ def tile_moe_duo_gelu_kernel(tc, x_words, x_scales, w1_words, w1_scales, wp_word
             for u in range(2):
                 nc.tensor.transpose(tr[:, u, :], h[:].bitcast(F32)[:, u * P:(u + 1) * P], ident[:])
             ht = work.tile([P, 4 * S], BF16, name="ht", align_bytes=64)
-            (nc.vector.tensor_copy if c in (0, 1) else nc.scalar.copy)(ht[:].bitcast(F32).rearrange("p (j u) -> p j u", u=2), tr[:].rearrange("p u j -> p j u"))
+            (nc.vector.tensor_copy if c == 1 else nc.scalar.copy)(ht[:].bitcast(F32).rearrange("p (j u) -> p j u", u=2), tr[:].rearrange("p u j -> p j u"))
             hts[c] = ht
 
         def second(c):
@@ -114,16 +117,15 @@ def tile_moe_duo_gelu_kernel(tc, x_words, x_scales, w1_words, w1_scales, wp_word
             ys[c] = y
 
         def empty(c):
-            nc.scalar.copy(yall[:, c * S:(c + 1) * S], ys[c][:])
+            row = keep.tile([P, S], F32, name="row%d" % c, tag="h%d" % ((c + 1) % TILES), align_bytes=64)
+            (nc.vector.tensor_copy if c == 0 else nc.scalar.copy)(row[:], ys[c][:])
+            rows[c] = row
 
         def scatter(c):
-            for c0, c1 in SCATTERS:
-                if c1 - 1 == c:
-                    cols = slice(c0 * S, c1 * S)
-                    nc.vector.tensor_tensor(res[:].indirect(lists[0][:, c0 * LC:c1 * LC]), yall[:, cols], g[:, cols], mybir.AluOpType.mult)
+            nc.vector.tensor_tensor(res[:].indirect(lists[0][:, c * LC:(c + 1) * LC]), rows[c][:], g[:, c * S:(c + 1) * S], mybir.AluOpType.mult)
 
-        stages = ((front, 0), (second, 1), (empty, 2), (scatter, 3))
-        for step in range(TILES + 3):
+        stages = ((scatter, 4), (empty, 3), (second, 2), (front, 1), (gather, 0))
+        for step in range(TILES + 4):
             for stage, lag in stages:
                 if 0 <= step - lag < TILES:
                     stage(step - lag)

@@ -22,8 +22,8 @@ LC = S // 16
 PIECES = ((0, 1), (1, 2), (2, 4))
 
 
-def load_plane(queue, plane, rows):
-    for q in range(4):
+def load_plane(queues, plane, rows):
+    for q, queue in enumerate(queues):
         queue.dma_start(out=plane[32 * q:32 * q + 4, :, :], in_=rows[:, 4 * q:4 * q + 4, :].rearrange("e r n -> r e n"))
 
 
@@ -32,7 +32,6 @@ def tile_moe_duo_gelu_kernel(tc, x_words, x_scales, w1_words, w1_scales, wp_word
     with ExitStack() as ctx:
         keep = ctx.enter_context(tc.tile_pool(name="keep", bufs=1))
         work = ctx.enter_context(tc.tile_pool(name="work", bufs=TILES))
-        ring = ctx.enter_context(tc.tile_pool(name="ring", bufs=2))
         pre_pool = ctx.enter_context(tc.psum_pool(name="pre", bufs=2))
         tr_pool = ctx.enter_context(tc.psum_pool(name="tr", bufs=2))
         y_pool = ctx.enter_context(tc.psum_pool(name="y", bufs=4))
@@ -44,7 +43,6 @@ def tile_moe_duo_gelu_kernel(tc, x_words, x_scales, w1_words, w1_scales, wp_word
         ws = [keep.tile([P, E, H], U8, name="ws%d" % a, align_bytes=64) for a in range(2)]
         w2w = keep.tile([P, E, 2 * N], U8, name="w2w", align_bytes=64)
         w2s = keep.tile([P, E, N], U8, name="w2s", align_bytes=64)
-        g = keep.tile([P, E * C], F32, name="g")
         res = keep.tile([P, T], F32, name="res")
         ident = keep.tile([P, P], F32, name="ident")
 
@@ -60,29 +58,31 @@ def tile_moe_duo_gelu_kernel(tc, x_words, x_scales, w1_words, w1_scales, wp_word
         for q in range(4):
             load_token_scales(nc.scalar if q else nc.sync, q)
         nc.scalar.dma_start(out=xw[:], in_=x_words[0].rearrange("p n t -> p (n t)").bitcast(I32))
-        make_identity(nc, ident[:])
-        for a, (queue, words) in enumerate(((nc.sync, w1_words), (nc.gpsimd, wp_words))):
-            queue.dma_start(out=ww[a][:].bitcast(I32), in_=words.rearrange("e s p n -> p (e s) n").bitcast(I32))
-        for a, queue, scales in ((0, nc.scalar, w1_scales), (1, nc.sync, wp_scales)):
-            load_plane(queue, ws[a][:].bitcast(I32), scales.rearrange("e s r n -> (e s) r n").bitcast(I32))
-        load_plane(nc.sync, w2s[:].bitcast(I32), w2_scales.rearrange("e s r n -> (e s) r n").bitcast(I32))
+        for a, queue, packed in ((0, nc.sync, w1_words), (1, nc.gpsimd, wp_words)):
+            queue.dma_start(out=ww[a][:].bitcast(I32), in_=packed.rearrange("e s p n -> p (e s) n").bitcast(I32))
+        nc.vector.memset(ident[:], 0.0)
+        make_identity(nc, ident[:], nomemset=True)
+        for a, queues, rows in ((0, [nc.sync, nc.scalar] * 2, w1_scales), (1, [nc.sync, nc.scalar] * 2, wp_scales)):
+            load_plane(queues, ws[a][:].bitcast(I32), rows.rearrange("e s r n -> (e s) r n").bitcast(I32))
+        load_plane([nc.sync] * 4, w2s[:].bitcast(I32), w2_scales.rearrange("e s r n -> (e s) r n").bitcast(I32))
         nc.sync.dma_start(out=w2w[:].bitcast(I32), in_=w2_words.rearrange("e s p n -> p (e s) n").bitcast(I32))
-        nc.sync.dma_start(out=g[:], in_=gate)
 
-        gathered = {}
+        words, scales = {}, {}
 
         def gather(c):
+            if c % 2 == 0:
+                for a in range(2):
+                    tag = "gs%d" % a if c == 0 else ("gw1_0", "gw0_1")[a]
+                    gs = keep.tile([P, 2 * S], U8, name="gs%d_%d" % (a, c), tag=tag, align_bytes=64)
+                    nc.vector.tensor_copy(gs[:], xs[:].indirect(lists[a][:, c * LC:(c + 2) * LC]))
+                    scales[c, a], scales[c + 1, a] = gs[:, :S], gs[:, S:]
             for c0, c1 in PIECES:
                 if c0 == c:
                     for a in range(2):
-                        sel = lists[a][:, c0 * LC:c1 * LC]
-                        gw = keep.tile([P, (c1 - c0) * S], U32, name="gw%d_%d" % (a, c0), align_bytes=64)
-                        gs = ring.tile([P, (c1 - c0) * S], U8, name="gs%d" % a, align_bytes=64)
-                        nc.vector.tensor_copy(gs[:], xs[:].indirect(sel))
-                        nc.vector.tensor_copy(gw[:], xw[:].bitcast(U32).indirect(sel))
+                        gw = keep.tile([P, (c1 - c0) * S], U32, name="gw%d_%d" % (a, c0), tag="gw%d_%d" % (a, c0), align_bytes=64)
+                        nc.vector.tensor_copy(gw[:], xw[:].bitcast(U32).indirect(lists[a][:, c0 * LC:c1 * LC]))
                         for t in range(c0, c1):
-                            cols = slice((t - c0) * S, (t - c0 + 1) * S)
-                            gathered[t, a] = (gw[:, cols], gs[:, cols])
+                            words[t, a] = gw[:, (t - c0) * S:(t - c0 + 1) * S]
 
         hts, ys = {}, {}
         rows = {}
@@ -91,7 +91,7 @@ def tile_moe_duo_gelu_kernel(tc, x_words, x_scales, w1_words, w1_scales, wp_word
             e = c * S // C
             pre = pre_pool.tile([P, H], F32, name="pre")
             for a in range(2):
-                gw, gs = gathered[c, a]
+                gw, gs = words[c, a], scales[c, a]
                 nc.tensor.matmul_mx(out=pre[:], lhsT=gw.bitcast(FP8X4), lhsT_scale=gs,
                                     rhs=ww[a][:, e, :].bitcast(FP4X4), rhs_scale=ws[a][:, e, :],
                                     start=(a == 0), stop=(a == 1))
@@ -121,7 +121,13 @@ def tile_moe_duo_gelu_kernel(tc, x_words, x_scales, w1_words, w1_scales, wp_word
             (nc.vector.tensor_copy if c == 0 else nc.scalar.copy)(row[:], ys[c][:])
             rows[c] = row
 
+        gates = {}
+
         def scatter(c):
+            if c == 0:
+                gates[0] = keep.tile([P, E * C], F32, name="g", tag="gw0_0", align_bytes=64)
+                nc.sync.dma_start(out=gates[0][:], in_=gate)
+            g = gates[0]
             nc.vector.tensor_tensor(res[:].indirect(lists[0][:, c * LC:(c + 1) * LC]), rows[c][:], g[:, c * S:(c + 1) * S], mybir.AluOpType.mult)
 
         stages = ((scatter, 4), (empty, 3), (second, 2), (front, 1), (gather, 0))

@@ -43,6 +43,7 @@ def tile_moe_duo_gelu_kernel(tc, x_words, x_scales, w1_words, w1_scales, wp_word
         ws = [keep.tile([P, E, H], U8, name="ws%d" % a, align_bytes=64) for a in range(2)]
         w2w = keep.tile([P, E, 2 * N], U8, name="w2w", align_bytes=64)
         w2s = keep.tile([P, E, N], U8, name="w2s", align_bytes=64)
+        g = keep.tile([P, E * C], F32, name="g")
         res = keep.tile([P, T], F32, name="res")
         ident = keep.tile([P, P], F32, name="ident")
 
@@ -58,21 +59,23 @@ def tile_moe_duo_gelu_kernel(tc, x_words, x_scales, w1_words, w1_scales, wp_word
         for q in range(4):
             load_token_scales(nc.scalar if q else nc.sync, q)
         nc.scalar.dma_start(out=xw[:], in_=x_words[0].rearrange("p n t -> p (n t)").bitcast(I32))
-        for a, queue, packed in ((0, nc.sync, w1_words), (1, nc.gpsimd, wp_words)):
-            queue.dma_start(out=ww[a][:].bitcast(I32), in_=packed.rearrange("e s p n -> p (e s) n").bitcast(I32))
+        nc.sync.dma_start(out=ww[0][:, 0, :].bitcast(I32), in_=w1_words[0, 0].bitcast(I32))
+        nc.gpsimd.dma_start(out=ww[1][:].bitcast(I32), in_=wp_words.rearrange("e s p n -> p (e s) n").bitcast(I32))
         nc.vector.memset(ident[:], 0.0)
         make_identity(nc, ident[:], nomemset=True)
         for a, queues, rows in ((0, [nc.sync, nc.scalar] * 2, w1_scales), (1, [nc.sync, nc.scalar] * 2, wp_scales)):
             load_plane(queues, ws[a][:].bitcast(I32), rows.rearrange("e s r n -> (e s) r n").bitcast(I32))
+        nc.sync.dma_start(out=ww[0][:, 1, :].bitcast(I32), in_=w1_words[1, 0].bitcast(I32))
         load_plane([nc.sync] * 4, w2s[:].bitcast(I32), w2_scales.rearrange("e s r n -> (e s) r n").bitcast(I32))
         nc.sync.dma_start(out=w2w[:].bitcast(I32), in_=w2_words.rearrange("e s p n -> p (e s) n").bitcast(I32))
+        nc.sync.dma_start(out=g[:], in_=gate)
 
         words, scales = {}, {}
 
         def gather(c):
             if c % 2 == 0:
                 for a in range(2):
-                    tag = "gs%d" % a if c == 0 else ("gw1_0", "gw0_1")[a]
+                    tag = "gs%d" % a if c == 0 else "gw%d_0" % a
                     gs = keep.tile([P, 2 * S], U8, name="gs%d_%d" % (a, c), tag=tag, align_bytes=64)
                     nc.vector.tensor_copy(gs[:], xs[:].indirect(lists[a][:, c * LC:(c + 2) * LC]))
                     scales[c, a], scales[c + 1, a] = gs[:, :S], gs[:, S:]
@@ -90,11 +93,12 @@ def tile_moe_duo_gelu_kernel(tc, x_words, x_scales, w1_words, w1_scales, wp_word
         def front(c):
             e = c * S // C
             pre = pre_pool.tile([P, H], F32, name="pre")
-            for a in range(2):
+            order = (1, 0) if c == 1 else (0, 1)
+            for a in order:
                 gw, gs = words[c, a], scales[c, a]
                 nc.tensor.matmul_mx(out=pre[:], lhsT=gw.bitcast(FP8X4), lhsT_scale=gs,
                                     rhs=ww[a][:, e, :].bitcast(FP4X4), rhs_scale=ws[a][:, e, :],
-                                    start=(a == 0), stop=(a == 1))
+                                    start=(a == order[0]), stop=(a == order[1]))
             h = keep.tile([P, H], BF16, name="h%d" % c, tag="h%d" % c, align_bytes=64)
             nc.scalar.activation(h[:].rearrange("p (u m d) -> p u m d", u=2, d=2),
                                  pre[:].rearrange("p (m u d) -> p u m d", u=2, d=2),
@@ -121,13 +125,7 @@ def tile_moe_duo_gelu_kernel(tc, x_words, x_scales, w1_words, w1_scales, wp_word
             (nc.vector.tensor_copy if c == 0 else nc.scalar.copy)(row[:], ys[c][:])
             rows[c] = row
 
-        gates = {}
-
         def scatter(c):
-            if c == 0:
-                gates[0] = keep.tile([P, E * C], F32, name="g", tag="gw0_0", align_bytes=64)
-                nc.sync.dma_start(out=gates[0][:], in_=gate)
-            g = gates[0]
             nc.vector.tensor_tensor(res[:].indirect(lists[0][:, c * LC:(c + 1) * LC]), rows[c][:], g[:, c * S:(c + 1) * S], mybir.AluOpType.mult)
 
         stages = ((scatter, 4), (empty, 3), (second, 2), (front, 1), (gather, 0))

@@ -19,7 +19,6 @@ P = 128
 S = 128
 TILES = E * C // S
 LC = S // 16
-PIECES = ((0, 1), (1, 2), (2, 4))
 
 
 def load_plane(queues, plane, rows):
@@ -63,8 +62,8 @@ def tile_moe_duo_gelu_kernel(tc, x_words, x_scales, w1_words, w1_scales, wp_word
         nc.gpsimd.dma_start(out=ww[1][:].bitcast(I32), in_=wp_words.rearrange("e s p n -> p (e s) n").bitcast(I32))
         nc.vector.memset(ident[:], 0.0)
         make_identity(nc, ident[:], nomemset=True)
-        for a, queues, rows in ((0, [nc.sync, nc.scalar] * 2, w1_scales), (1, [nc.sync, nc.scalar] * 2, wp_scales)):
-            load_plane(queues, ws[a][:].bitcast(I32), rows.rearrange("e s r n -> (e s) r n").bitcast(I32))
+        for a, rows in ((0, w1_scales), (1, wp_scales)):
+            load_plane([nc.sync, nc.scalar] * 2, ws[a][:].bitcast(I32), rows.rearrange("e s r n -> (e s) r n").bitcast(I32))
         nc.sync.dma_start(out=ww[0][:, 1, :].bitcast(I32), in_=w1_words[1, 0].bitcast(I32))
         load_plane([nc.sync] * 4, w2s[:].bitcast(I32), w2_scales.rearrange("e s r n -> (e s) r n").bitcast(I32))
         nc.sync.dma_start(out=w2w[:].bitcast(I32), in_=w2_words.rearrange("e s p n -> p (e s) n").bitcast(I32))
@@ -72,66 +71,85 @@ def tile_moe_duo_gelu_kernel(tc, x_words, x_scales, w1_words, w1_scales, wp_word
 
         words, scales = {}, {}
 
-        def gather(c):
-            if c % 2 == 0:
-                for a in range(2):
-                    tag = "gs%d" % a if c == 0 else "gw%d_0" % a
-                    gs = keep.tile([P, 2 * S], U8, name="gs%d_%d" % (a, c), tag=tag, align_bytes=64)
-                    nc.vector.tensor_copy(gs[:], xs[:].indirect(lists[a][:, c * LC:(c + 2) * LC]))
-                    scales[c, a], scales[c + 1, a] = gs[:, :S], gs[:, S:]
-            for c0, c1 in PIECES:
-                if c0 == c:
-                    for a in range(2):
-                        gw = keep.tile([P, (c1 - c0) * S], U32, name="gw%d_%d" % (a, c0), tag="gw%d_%d" % (a, c0), align_bytes=64)
-                        nc.vector.tensor_copy(gw[:], xw[:].bitcast(U32).indirect(lists[a][:, c0 * LC:c1 * LC]))
-                        for t in range(c0, c1):
-                            words[t, a] = gw[:, (t - c0) * S:(t - c0 + 1) * S]
+        def gather_scales(a, e, tag):
+            gs = keep.tile([P, C], U8, name="gs%d_%d" % (a, e), tag=tag, align_bytes=64)
+            nc.vector.tensor_copy(gs[:], xs[:].indirect(lists[a][:, 2 * e * LC:2 * (e + 1) * LC]))
+            scales[2 * e, a], scales[2 * e + 1, a] = gs[:, :S], gs[:, S:]
 
-        hts, ys = {}, {}
-        rows = {}
+        def gather_words(a, c0, c1, tag):
+            gw = keep.tile([P, (c1 - c0) * S], U32, name="gw%d_%d" % (a, c0), tag=tag, align_bytes=64)
+            nc.vector.tensor_copy(gw[:], xw[:].bitcast(U32).indirect(lists[a][:, c0 * LC:c1 * LC]))
+            for c in range(c0, c1):
+                words[c, a] = gw[:, (c - c0) * S:(c - c0 + 1) * S]
 
-        def front(c):
+        pres, hs, hts, ys, rows = {}, {}, {}, {}, {}
+
+        def first_pass(c, a, opens):
+            if opens:
+                pres[c] = pre_pool.tile([P, H], F32, name="pre")
             e = c * S // C
-            pre = pre_pool.tile([P, H], F32, name="pre")
-            order = (1, 0) if c == 1 else (0, 1)
-            for a in order:
-                gw, gs = words[c, a], scales[c, a]
-                nc.tensor.matmul_mx(out=pre[:], lhsT=gw.bitcast(FP8X4), lhsT_scale=gs,
-                                    rhs=ww[a][:, e, :].bitcast(FP4X4), rhs_scale=ws[a][:, e, :],
-                                    start=(a == order[0]), stop=(a == order[1]))
+            nc.tensor.matmul_mx(out=pres[c][:], lhsT=words[c, a].bitcast(FP8X4), lhsT_scale=scales[c, a],
+                                rhs=ww[a][:, e, :].bitcast(FP4X4), rhs_scale=ws[a][:, e, :],
+                                start=opens, stop=not opens)
+
+        def activate(c):
             h = keep.tile([P, H], BF16, name="h%d" % c, tag="h%d" % c, align_bytes=64)
             nc.scalar.activation(h[:].rearrange("p (u m d) -> p u m d", u=2, d=2),
-                                 pre[:].rearrange("p (m u d) -> p u m d", u=2, d=2),
+                                 pres[c][:].rearrange("p (m u d) -> p u m d", u=2, d=2),
                                  mybir.ActivationFunctionType.Gelu_apprx_tanh)
+            hs[c] = h
+
+        def turn(c):
             tr = tr_pool.tile([P, 2, S], F32, name="tr")
             for u in range(2):
-                nc.tensor.transpose(tr[:, u, :], h[:].bitcast(F32)[:, u * P:(u + 1) * P], ident[:])
+                nc.tensor.transpose(tr[:, u, :], hs[c][:].bitcast(F32)[:, u * P:(u + 1) * P], ident[:])
             ht = work.tile([P, 4 * S], BF16, name="ht", align_bytes=64)
-            (nc.vector.tensor_copy if c == 1 else nc.scalar.copy)(ht[:].bitcast(F32).rearrange("p (j u) -> p j u", u=2), tr[:].rearrange("p u j -> p j u"))
+            (nc.vector.tensor_copy if c < 2 else nc.scalar.copy)(ht[:].bitcast(F32).rearrange("p (j u) -> p j u", u=2), tr[:].rearrange("p u j -> p j u"))
             hts[c] = ht
 
         def second(c):
             e = c * S // C
             hq = work.tile([P, S], U32, name="hq", align_bytes=64)
-            hs = work.tile([P, S], U8, name="hs", align_bytes=64)
-            nc.vector.quantize_mx(out=hq[:].bitcast(FP8X4), scales=hs[:], in_=hts[c][:])
+            hscale = work.tile([P, S], U8, name="hscale", align_bytes=64)
+            nc.vector.quantize_mx(out=hq[:].bitcast(FP8X4), scales=hscale[:], in_=hts[c][:])
             y = y_pool.tile([P, S], F32, name="y")
             nc.tensor.matmul_mx(out=y[:], lhsT=w2w[:, e, :].bitcast(FP4X4), lhsT_scale=w2s[:, e, :],
-                                rhs=hq[:].bitcast(FP8X4), rhs_scale=hs[:], start=True, stop=True)
+                                rhs=hq[:].bitcast(FP8X4), rhs_scale=hscale[:], start=True, stop=True)
             ys[c] = y
 
-        def empty(c):
-            row = keep.tile([P, S], F32, name="row%d" % c, tag="h%d" % ((c + 1) % TILES), align_bytes=64)
-            (nc.vector.tensor_copy if c == 0 else nc.scalar.copy)(row[:], ys[c][:])
-            rows[c] = row
+        def finish(j0, j1, tag):
+            row = keep.tile([P, j1 - j0], F32, name="row%d" % j0, tag=tag, align_bytes=64)
+            for c in range(j0 // S, (j1 - 1) // S + 1):
+                lo, hi = max(j0, c * S), min(j1, (c + 1) * S)
+                (nc.vector.tensor_copy if c == 0 else nc.scalar.copy)(row[:, lo - j0:hi - j0], ys[c][:, lo - c * S:hi - c * S])
+            nc.vector.tensor_tensor(res[:].indirect(lists[0][:, j0 // 16:j1 // 16]), row[:], g[:, j0:j1], mybir.AluOpType.mult)
 
-        def scatter(c):
-            nc.vector.tensor_tensor(res[:].indirect(lists[0][:, c * LC:(c + 1) * LC]), rows[c][:], g[:, c * S:(c + 1) * S], mybir.AluOpType.mult)
-
-        stages = ((scatter, 4), (empty, 3), (second, 2), (front, 1), (gather, 0))
-        for step in range(TILES + 4):
-            for stage, lag in stages:
-                if 0 <= step - lag < TILES:
-                    stage(step - lag)
+        for a in range(2):
+            gather_scales(a, 0, "gs%d" % a)
+        for c in range(2):
+            for a in range(2):
+                gather_words(a, c, c + 1, "gw%d_%d" % (a, c))
+        for c, order in ((0, (0, 1)), (1, (1, 0))):
+            for a in order:
+                first_pass(c, a, a == order[0])
+            activate(c)
+        for a in range(2):
+            gather_words(a, 2, 4, "gw%d_2" % a)
+        for a in range(2):
+            gather_scales(a, 1, "gw%d_0" % a)
+        turn(0)
+        for c in (2, 3):
+            second(c - 2)
+            first_pass(c, 0, True)
+            first_pass(c, 1, False)
+            activate(c)
+            turn(c - 1)
+        finish(0, S, "h1")
+        second(2)
+        finish(S, 2 * S, "h2")
+        turn(3)
+        second(3)
+        finish(2 * S, 3 * S, "h3")
+        finish(3 * S, 4 * S, "h0")
 
         nc.sync.dma_start(out=out, in_=res[:])

@@ -26,6 +26,10 @@ def load_plane(queues, plane, rows):
         queue.dma_start(out=plane[32 * q:32 * q + 4, :, :], in_=rows[:, 4 * q:4 * q + 4, :].rearrange("e r n -> r e n"))
 
 
+def repeat_rows(rows, times):
+    return rows.unsqueeze(0).broadcast_to([times, rows.shape[0], rows.shape[1]])
+
+
 def tile_moe_duo_gelu_kernel(tc, x_words, x_scales, w1_words, w1_scales, wp_words, wp_scales, w2_words, w2_scales, gate, offs, offs2, out):
     nc = tc.nc
     with ExitStack() as ctx:
@@ -59,13 +63,17 @@ def tile_moe_duo_gelu_kernel(tc, x_words, x_scales, w1_words, w1_scales, wp_word
             load_token_scales(nc.scalar if q else nc.sync, q)
         nc.scalar.dma_start(out=xw[:], in_=x_words[0].rearrange("p n t -> p (n t)").bitcast(I32))
         nc.sync.dma_start(out=ww[0][:, 0, :].bitcast(I32), in_=w1_words[0, 0].bitcast(I32))
-        nc.gpsimd.dma_start(out=ww[1][:].bitcast(I32), in_=wp_words.rearrange("e s p n -> p (e s) n").bitcast(I32))
+        nc.gpsimd.dma_start(out=ww[1][:, 0, :].bitcast(I32), in_=wp_words[0, 0].bitcast(I32))
         nc.vector.memset(ident[:], 0.0)
         make_identity(nc, ident[:], nomemset=True)
         for a, rows in ((0, w1_scales), (1, wp_scales)):
             load_plane([nc.sync, nc.scalar] * 2, ws[a][:].bitcast(I32), rows.rearrange("e s r n -> (e s) r n").bitcast(I32))
         nc.sync.dma_start(out=ww[0][:, 1, :].bitcast(I32), in_=w1_words[1, 0].bitcast(I32))
-        load_plane([nc.sync] * 4, w2s[:].bitcast(I32), w2_scales.rearrange("e s r n -> (e s) r n").bitcast(I32))
+        nc.sync.dma_start(out=ww[1][:, 1, :].bitcast(I32), in_=wp_words[1, 0].bitcast(I32))
+        w2_rows = w2_scales.rearrange("e s r n -> (e s r) n").bitcast(I32)
+        nc.sync.dma_start(out=w2s[0:112, 0, :].bitcast(I32), in_=repeat_rows(w2_rows[0:28, :], 4))
+        nc.sync.dma_start(out=w2s[0:4, 1, :].bitcast(I32), in_=w2_rows[16:20, :])
+        nc.sync.dma_start(out=w2s[16:100, 1, :].bitcast(I32), in_=repeat_rows(w2_rows[4:32, :], 3))
         nc.sync.dma_start(out=w2w[:].bitcast(I32), in_=w2_words.rearrange("e s p n -> p (e s) n").bitcast(I32))
         nc.sync.dma_start(out=g[:], in_=gate)
 

@@ -112,7 +112,7 @@ def tile_moe_duo_gelu_kernel(tc, x_words, x_scales, w1_words, w1_scales, wp_word
             for u in range(2):
                 nc.tensor.transpose(tr[:, u, :], hs[c][:].bitcast(F32)[:, u * P:(u + 1) * P], ident[:])
             ht = work.tile([P, 4 * S], BF16, name="ht", align_bytes=64)
-            (nc.vector.tensor_copy if c < 2 else nc.scalar.copy)(ht[:].bitcast(F32).rearrange("p (j u) -> p j u", u=2), tr[:].rearrange("p u j -> p j u"))
+            (nc.scalar.copy if c == 2 else nc.vector.tensor_copy)(ht[:].bitcast(F32).rearrange("p (j u) -> p j u", u=2), tr[:].rearrange("p u j -> p j u"))
             hts[c] = ht
 
         def second(c):
@@ -153,11 +153,15 @@ def tile_moe_duo_gelu_kernel(tc, x_words, x_scales, w1_words, w1_scales, wp_word
             activate(c)
             turn(c - 1)
         finish(0, S, "h1")
+        row1 = keep.tile([P, S], F32, name="row1", tag="h2", align_bytes=64)
+        nc.vector.tensor_tensor(row1[:], ys[1][:], g[:, S:2 * S], mybir.AluOpType.mult)
+        nc.scalar.activation(res[:].indirect(lists[0][:, LC:2 * LC]), row1[:], mybir.ActivationFunctionType.Copy)
         second(2)
-        finish(S, 2 * S, "h2")
         turn(3)
+        row2 = keep.tile([P, S], F32, name="row2", tag="h3", align_bytes=64)
+        nc.vector.tensor_tensor(row2[:], ys[2][:], g[:, 2 * S:3 * S], mybir.AluOpType.mult)
         second(3)
-        finish(2 * S, 3 * S, "h3")
+        nc.vector.tensor_copy(res[:].indirect(lists[0][:, 2 * LC:3 * LC]), row2[:])
         finish(3 * S, 4 * S, "h0")
 
         nc.sync.dma_start(out=out, in_=res[:])

@@ -50,8 +50,13 @@ def tile_moe_duo_gelu_kernel(tc, x_words, x_scales, w1_words, w1_scales, wp_word
         res = keep.tile([P, T], F32, name="res")
         ident = keep.tile([P, P], F32, name="ident")
 
+        def clear(flat):
+            cut = flat.shape[1] // 2 + 1
+            nc.vector.memset(flat[:, :cut], 0)
+            nc.vector.memset(flat[:, cut:], 0)
+
         for plane in (ws[0], ws[1], w2s):
-            nc.vector.memset(plane[:].bitcast(I32), 0)
+            clear(plane[:].rearrange("p e n -> p (e n)").bitcast(I32))
 
         def load_token_scales(queue, q):
             rows = x_scales[0, 4 * q:4 * q + 4, :].bitcast(I32)
@@ -64,7 +69,7 @@ def tile_moe_duo_gelu_kernel(tc, x_words, x_scales, w1_words, w1_scales, wp_word
         nc.scalar.dma_start(out=xw[:], in_=x_words[0].rearrange("p n t -> p (n t)").bitcast(I32))
         nc.sync.dma_start(out=ww[0][:, 0, :].bitcast(I32), in_=w1_words[0, 0].bitcast(I32))
         nc.gpsimd.dma_start(out=ww[1][:, 0, :].bitcast(I32), in_=wp_words[0, 0].bitcast(I32))
-        nc.vector.memset(ident[:], 0.0)
+        clear(ident[:])
         make_identity(nc, ident[:], nomemset=True)
         for a, rows in ((0, w1_scales), (1, wp_scales)):
             load_plane([nc.sync, nc.scalar] * 2, ws[a][:].bitcast(I32), rows.rearrange("e s r n -> (e s) r n").bitcast(I32))
@@ -72,10 +77,10 @@ def tile_moe_duo_gelu_kernel(tc, x_words, x_scales, w1_words, w1_scales, wp_word
         nc.sync.dma_start(out=ww[1][:, 1, :].bitcast(I32), in_=wp_words[1, 0].bitcast(I32))
         w2_rows = w2_scales.rearrange("e s r n -> (e s r) n").bitcast(I32)
         nc.sync.dma_start(out=w2s[0:112, 0, :].bitcast(I32), in_=repeat_rows(w2_rows[0:28, :], 4))
-        nc.sync.dma_start(out=w2s[0:4, 1, :].bitcast(I32), in_=w2_rows[16:20, :])
-        nc.sync.dma_start(out=w2s[16:100, 1, :].bitcast(I32), in_=repeat_rows(w2_rows[4:32, :], 3))
         nc.sync.dma_start(out=w2w[:].bitcast(I32), in_=w2_words.rearrange("e s p n -> p (e s) n").bitcast(I32))
         nc.sync.dma_start(out=g[:], in_=gate)
+        nc.sync.dma_start(out=w2s[0:4, 1, :].bitcast(I32), in_=w2_rows[16:20, :])
+        nc.sync.dma_start(out=w2s[16:100, 1, :].bitcast(I32), in_=repeat_rows(w2_rows[4:32, :], 3))
 
         words, scales = {}, {}
 

@@ -142,21 +142,37 @@ def tile_moe_duo_gelu_kernel(tc, x_words, x_scales, w1_words, w1_scales, wp_word
         for c in range(2):
             for a in range(2):
                 gather_words(a, c, c + 1, "gw%d_%d" % (a, c))
-        for c, order in ((0, (0, 1)), (1, (1, 0))):
-            for a in order:
-                first_pass(c, a, a == order[0])
-            activate(c)
+        def first_in_halves(c, pools):
+            e = c * S // C
+            hs[c] = keep.tile([P, H], BF16, name="h%d" % c, tag="h%d" % c, align_bytes=64)
+            for half, (pool, name) in enumerate(pools):
+                pre = pool.tile([P, H // 2], F32, name=name)
+                for a in range(2):
+                    nc.tensor.matmul_mx(out=pre[:], lhsT=words[c, a].bitcast(FP8X4), lhsT_scale=scales[c, a],
+                                        rhs=ww[a][:, e, half * H:(half + 1) * H].bitcast(FP4X4),
+                                        rhs_scale=ws[a][:, e, half * H // 2:(half + 1) * H // 2],
+                                        start=a == 0, stop=a == 1)
+                nc.scalar.activation(hs[c][:].rearrange("p (u k m d) -> p k u m d", u=2, k=2, d=2)[:, half],
+                                     pre[:].rearrange("p (m u d) -> p u m d", u=2, d=2),
+                                     mybir.ActivationFunctionType.Gelu_apprx_tanh)
+
+        first_in_halves(0, ((y_pool, "y"), (pre_pool, "pre")))
+        for a in (1, 0):
+            first_pass(1, a, a == 1)
+        activate(1)
         for a in range(2):
             gather_words(a, 2, 4, "gw%d_2" % a)
         for a in range(2):
             gather_scales(a, 1, "gw%d_0" % a)
         turn(0)
-        for c in (2, 3):
-            second(c - 2)
-            first_pass(c, 0, True)
-            first_pass(c, 1, False)
-            activate(c)
-            turn(c - 1)
+        second(0)
+        first_pass(2, 0, True)
+        first_pass(2, 1, False)
+        activate(2)
+        turn(1)
+        second(1)
+        first_in_halves(3, ((pre_pool, "pre"), (tr_pool, "tr")))
+        turn(2)
         finish(0, S, "h1")
         row1 = keep.tile([P, S], F32, name="row1", tag="h2", align_bytes=64)
         nc.vector.tensor_tensor(row1[:], ys[1][:], g[:, S:2 * S], mybir.AluOpType.mult)

@@ -72,7 +72,7 @@ def tile_moe_duo_gelu_kernel(tc, x_words, x_scales, w1_words, w1_scales, wp_word
         clear(ident[:])
         make_identity(nc, ident[:], nomemset=True)
         for a, rows in ((0, w1_scales), (1, wp_scales)):
-            load_plane([nc.sync, nc.scalar] * 2, ws[a][:].bitcast(I32), rows.rearrange("e s r n -> (e s) r n").bitcast(I32))
+            load_plane([nc.sync, nc.scalar, nc.sync, nc.sync if a else nc.scalar], ws[a][:].bitcast(I32), rows.rearrange("e s r n -> (e s) r n").bitcast(I32))
         nc.sync.dma_start(out=ww[0][:, 1, :].bitcast(I32), in_=w1_words[1, 0].bitcast(I32))
         nc.sync.dma_start(out=ww[1][:, 1, :].bitcast(I32), in_=wp_words[1, 0].bitcast(I32))
         w2_rows = w2_scales.rearrange("e s r n -> (e s r) n").bitcast(I32)

@@ -1,7 +1,6 @@
 from contextlib import ExitStack
 
 import concourse.mybir as mybir
-from concourse.masks import make_identity
 
 K, T, E, C, H, N = 512, 512, 2, 256, 512, 128
 FLOPS = 2 * E * C * (2 * K * H + H * N)
@@ -14,20 +13,12 @@ U16 = mybir.dt.uint16
 U8 = mybir.dt.uint8
 FP8X4 = mybir.dt.float8_e4m3fn_x4
 FP4X4 = mybir.dt.float4_e2m1fn_x4
+GELU = mybir.ActivationFunctionType.Gelu_apprx_tanh
 
 P = 128
 S = 128
 TILES = E * C // S
 LC = S // 16
-
-
-def load_plane(queues, plane, rows):
-    for q, queue in enumerate(queues):
-        queue.dma_start(out=plane[32 * q:32 * q + 4, :, :], in_=rows[:, 4 * q:4 * q + 4, :].rearrange("e r n -> r e n"))
-
-
-def repeat_rows(rows, times):
-    return rows.unsqueeze(0).broadcast_to([times, rows.shape[0], rows.shape[1]])
 
 
 def tile_moe_duo_gelu_kernel(tc, x_words, x_scales, w1_words, w1_scales, wp_words, wp_scales, w2_words, w2_scales, gate, offs, offs2, out):
@@ -36,51 +27,75 @@ def tile_moe_duo_gelu_kernel(tc, x_words, x_scales, w1_words, w1_scales, wp_word
         keep = ctx.enter_context(tc.tile_pool(name="keep", bufs=1))
         work = ctx.enter_context(tc.tile_pool(name="work", bufs=TILES))
         pre_pool = ctx.enter_context(tc.psum_pool(name="pre", bufs=2))
-        tr_pool = ctx.enter_context(tc.psum_pool(name="tr", bufs=2))
         y_pool = ctx.enter_context(tc.psum_pool(name="y", bufs=4))
 
         xw = keep.tile([P, T], I32, name="xw", align_bytes=64)
         xs = keep.tile([P, T], U8, name="xs", align_bytes=64)
         lists = [keep.tile([P, E * C // 16], U16, name="list%d" % a) for a in range(2)]
-        ww = [keep.tile([P, E, 2 * H], U8, name="ww%d" % a, align_bytes=64) for a in range(2)]
-        ws = [keep.tile([P, E, H], U8, name="ws%d" % a, align_bytes=64) for a in range(2)]
+        raw_wp = keep.tile([P, E, 2 * H], U8, name="raw_wp", align_bytes=64)
+        raw_w1 = [keep.tile([P, 2 * H], U8, name="raw_w1%d" % e, align_bytes=64) for e in range(E)]
+        raw_w = {(1, 0): raw_wp[:, 0, :], (1, 1): raw_wp[:, 1, :], (0, 0): raw_w1[0][:], (0, 1): raw_w1[1][:]}
+        raw_s = [keep.tile([P, E, H], U8, name="raw_s%d" % a, align_bytes=64) for a in range(2)]
         w2w = keep.tile([P, E, 2 * N], U8, name="w2w", align_bytes=64)
         w2s = keep.tile([P, E, N], U8, name="w2s", align_bytes=64)
         g = keep.tile([P, E * C], F32, name="g")
         res = keep.tile([P, T], F32, name="res")
-        ident = keep.tile([P, P], F32, name="ident")
+        warm = keep.tile([P, 2], F32, name="warm")
 
         def clear(flat):
             cut = flat.shape[1] // 2 + 1
             nc.vector.memset(flat[:, :cut], 0)
             nc.vector.memset(flat[:, cut:], 0)
 
-        for plane in (ws[0], ws[1], w2s):
+        nc.vector.memset(warm[:, 0:1], 0.0)
+        clear(raw_s[0][:].rearrange("p e n -> p (e n)").bitcast(I32))
+        for plane in (raw_s[1], w2s):
             clear(plane[:].rearrange("p e n -> p (e n)").bitcast(I32))
 
         def load_token_scales(queue, q):
             rows = x_scales[0, 4 * q:4 * q + 4, :].bitcast(I32)
             queue.dma_start(out=xs[32 * q:32 * q + 32, :].bitcast(I32), in_=rows.unsqueeze(0).broadcast_to([8, 4, T // 4]))
 
+        def load_quadrant(queue, plane, scales, q):
+            rows = scales.rearrange("e s r n -> (e s) r n").bitcast(I32)
+            queue.dma_start(out=plane[:].bitcast(I32)[32 * q:32 * q + 4, :, :], in_=rows[:, 4 * q:4 * q + 4, :].rearrange("e r n -> r e n"))
+
+        nc.gpsimd.dma_start(out=raw_wp[:].bitcast(I32), in_=wp_words.rearrange("e s p n -> p (e s) n").bitcast(I32))
+        nc.gpsimd.dma_start(out=raw_w1[1][:].bitcast(I32), in_=w1_words[1, 0].bitcast(I32))
         nc.sync.dma_start(lists[0][:], offs)
         nc.sync.dma_start(lists[1][:], offs2)
         for q in range(4):
             load_token_scales(nc.scalar if q else nc.sync, q)
-        nc.scalar.dma_start(out=xw[:], in_=x_words[0].rearrange("p n t -> p (n t)").bitcast(I32))
-        nc.sync.dma_start(out=ww[0][:, 0, :].bitcast(I32), in_=w1_words[0, 0].bitcast(I32))
-        nc.gpsimd.dma_start(out=ww[1][:, 0, :].bitcast(I32), in_=wp_words[0, 0].bitcast(I32))
-        clear(ident[:])
-        make_identity(nc, ident[:], nomemset=True)
-        for a, rows in ((0, w1_scales), (1, wp_scales)):
-            load_plane([nc.sync, nc.scalar, nc.sync, nc.sync if a else nc.scalar], ws[a][:].bitcast(I32), rows.rearrange("e s r n -> (e s) r n").bitcast(I32))
-        nc.sync.dma_start(out=ww[0][:, 1, :].bitcast(I32), in_=w1_words[1, 0].bitcast(I32))
-        nc.sync.dma_start(out=ww[1][:, 1, :].bitcast(I32), in_=wp_words[1, 0].bitcast(I32))
-        w2_rows = w2_scales.rearrange("e s r n -> (e s r) n").bitcast(I32)
-        nc.sync.dma_start(out=w2s[0:112, 0, :].bitcast(I32), in_=repeat_rows(w2_rows[0:28, :], 4))
+        nc.sync.dma_start(out=xw[:], in_=x_words[0].rearrange("p n t -> p (n t)").bitcast(I32))
+        nc.scalar.dma_start(out=raw_w1[0][:].bitcast(I32), in_=w1_words[0, 0].bitcast(I32))
+        nc.scalar.activation(warm[:, 1:2], warm[:, 0:1], GELU)
+        for q in range(4):
+            load_quadrant(nc.scalar if q % 2 else nc.sync, raw_s[0], w1_scales, q)
+        for q in range(4):
+            load_quadrant(nc.scalar if q == 1 else nc.sync, raw_s[1], wp_scales, q)
         nc.sync.dma_start(out=w2w[:].bitcast(I32), in_=w2_words.rearrange("e s p n -> p (e s) n").bitcast(I32))
+        for q in (0, 2):
+            load_quadrant(nc.sync, w2s, w2_scales, q)
         nc.sync.dma_start(out=g[:], in_=gate)
-        nc.sync.dma_start(out=w2s[0:4, 1, :].bitcast(I32), in_=w2_rows[16:20, :])
-        nc.sync.dma_start(out=w2s[16:100, 1, :].bitcast(I32), in_=repeat_rows(w2_rows[4:32, :], 3))
+
+        ww, ws = {}, {}
+
+        def deal_words(a, e, to):
+            nc.scalar.copy(to.bitcast(U16).rearrange("p (t m) -> p t m", t=4), raw_w[a, e].bitcast(U16).rearrange("p (m t) -> p t m", t=4))
+            ww[a, e] = to
+
+        def deal_scales(a, e, to):
+            nc.gpsimd.tensor_copy(to.rearrange("p (t m) -> p t m", t=4), raw_s[a][:, e, :].rearrange("p (m t) -> p t m", t=4))
+            ws[a, e] = to
+
+        for a, e in ((0, 0), (1, 0), (1, 1), (0, 1)):
+            deal_words(a, e, keep.tile([P, 2 * H], U8, name="ww%d_%d" % (a, e), align_bytes=64)[:])
+            if e == 0 and a == 0:
+                for q in (1, 3):
+                    load_quadrant(nc.scalar, w2s, w2_scales, q)
+        for a, e in ((0, 0), (1, 0), (1, 1)):
+            deal_scales(a, e, keep.tile([P, H], U8, name="ws%d_%d" % (a, e), align_bytes=64)[:])
+        deal_scales(0, 1, raw_s[1][:, 0, :])
 
         words, scales = {}, {}
 
@@ -89,100 +104,62 @@ def tile_moe_duo_gelu_kernel(tc, x_words, x_scales, w1_words, w1_scales, wp_word
             nc.vector.tensor_copy(gs[:], xs[:].indirect(lists[a][:, 2 * e * LC:2 * (e + 1) * LC]))
             scales[2 * e, a], scales[2 * e + 1, a] = gs[:, :S], gs[:, S:]
 
-        def gather_words(a, c0, c1, tag):
-            gw = keep.tile([P, (c1 - c0) * S], U32, name="gw%d_%d" % (a, c0), tag=tag, align_bytes=64)
+        def gather_words(a, c0, c1):
+            gw = keep.tile([P, (c1 - c0) * S], U32, name="gw%d_%d" % (a, c0), align_bytes=64)
             nc.vector.tensor_copy(gw[:], xw[:].bitcast(U32).indirect(lists[a][:, c0 * LC:c1 * LC]))
             for c in range(c0, c1):
                 words[c, a] = gw[:, (c - c0) * S:(c - c0 + 1) * S]
 
-        pres, hs, hts, ys, rows = {}, {}, {}, {}, {}
+        gather_scales(0, 0, "gs0")
+        gather_scales(1, 0, "gs1")
+        gather_words(0, 0, 2)
+        gather_words(1, 0, 2)
+        gather_words(0, 2, 4)
+        gather_words(1, 2, 4)
+        gather_scales(0, 1, "raw_w10")
+        gather_scales(1, 1, "raw_wp")
 
-        def first_pass(c, a, opens):
-            if opens:
-                pres[c] = pre_pool.tile([P, H], F32, name="pre")
+        pres, hs, ys = {}, {}, {}
+
+        def first(c):
             e = c * S // C
-            nc.tensor.matmul_mx(out=pres[c][:], lhsT=words[c, a].bitcast(FP8X4), lhsT_scale=scales[c, a],
-                                rhs=ww[a][:, e, :].bitcast(FP4X4), rhs_scale=ws[a][:, e, :],
-                                start=opens, stop=not opens)
-
-        def activate(c):
-            h = keep.tile([P, H], BF16, name="h%d" % c, tag="h%d" % c, align_bytes=64)
-            nc.scalar.activation(h[:].rearrange("p (u m d) -> p u m d", u=2, d=2),
-                                 pres[c][:].rearrange("p (m u d) -> p u m d", u=2, d=2),
-                                 mybir.ActivationFunctionType.Gelu_apprx_tanh)
+            pre = pre_pool.tile([P, 4, S], F32, name="pre")
+            order = (1, 0) if c else (0, 1)
+            for a in order:
+                for t in range(4):
+                    nc.tensor.matmul_mx(out=pre[:, t, :], lhsT=ww[a, e][:, 2 * t * P:2 * (t + 1) * P].bitcast(FP4X4),
+                                        lhsT_scale=ws[a, e][:, t * P:(t + 1) * P],
+                                        rhs=words[c, a].bitcast(FP8X4), rhs_scale=scales[c, a],
+                                        start=a == order[0] and t == 0, stop=a == order[1] and t == 3)
+            h = work.tile([P, 4 * S], BF16, name="h", align_bytes=64)
+            nc.scalar.activation(h[:].rearrange("p (j t) -> p j t", t=4), pre[:].rearrange("p t j -> p j t"), GELU)
             hs[c] = h
-
-        def turn(c):
-            tr = tr_pool.tile([P, 2, S], F32, name="tr")
-            for u in range(2):
-                nc.tensor.transpose(tr[:, u, :], hs[c][:].bitcast(F32)[:, u * P:(u + 1) * P], ident[:])
-            ht = work.tile([P, 4 * S], BF16, name="ht", align_bytes=64)
-            (nc.scalar.copy if c == 2 else nc.vector.tensor_copy)(ht[:].bitcast(F32).rearrange("p (j u) -> p j u", u=2), tr[:].rearrange("p u j -> p j u"))
-            hts[c] = ht
 
         def second(c):
             e = c * S // C
             hq = work.tile([P, S], U32, name="hq", align_bytes=64)
             hscale = work.tile([P, S], U8, name="hscale", align_bytes=64)
-            nc.vector.quantize_mx(out=hq[:].bitcast(FP8X4), scales=hscale[:], in_=hts[c][:])
+            nc.vector.quantize_mx(out=hq[:].bitcast(FP8X4), scales=hscale[:], in_=hs[c][:])
             y = y_pool.tile([P, S], F32, name="y")
             nc.tensor.matmul_mx(out=y[:], lhsT=w2w[:, e, :].bitcast(FP4X4), lhsT_scale=w2s[:, e, :],
                                 rhs=hq[:].bitcast(FP8X4), rhs_scale=hscale[:], start=True, stop=True)
             ys[c] = y
 
-        def finish(j0, j1, tag):
-            row = keep.tile([P, j1 - j0], F32, name="row%d" % j0, tag=tag, align_bytes=64)
-            for c in range(j0 // S, (j1 - 1) // S + 1):
-                lo, hi = max(j0, c * S), min(j1, (c + 1) * S)
-                (nc.vector.tensor_copy if c == 0 else nc.scalar.copy)(row[:, lo - j0:hi - j0], ys[c][:, lo - c * S:hi - c * S])
-            nc.vector.tensor_tensor(res[:].indirect(lists[0][:, j0 // 16:j1 // 16]), row[:], g[:, j0:j1], mybir.AluOpType.mult)
+        def finish(c):
+            row = work.tile([P, S], F32, name="row", align_bytes=64)
+            if c == 0:
+                nc.vector.tensor_tensor(row[:], ys[c][:], g[:, :S], mybir.AluOpType.mult)
+            else:
+                nc.scalar.copy(row[:], ys[c][:])
+            return row
 
-        for a in range(2):
-            gather_scales(a, 0, "gs%d" % a)
-        for c in range(2):
-            for a in range(2):
-                gather_words(a, c, c + 1, "gw%d_%d" % (a, c))
-        def first_in_halves(c, pools):
-            e = c * S // C
-            hs[c] = keep.tile([P, H], BF16, name="h%d" % c, tag="h%d" % c, align_bytes=64)
-            for half, (pool, name) in enumerate(pools):
-                pre = pool.tile([P, H // 2], F32, name=name)
-                for a in range(2):
-                    nc.tensor.matmul_mx(out=pre[:], lhsT=words[c, a].bitcast(FP8X4), lhsT_scale=scales[c, a],
-                                        rhs=ww[a][:, e, half * H:(half + 1) * H].bitcast(FP4X4),
-                                        rhs_scale=ws[a][:, e, half * H // 2:(half + 1) * H // 2],
-                                        start=a == 0, stop=a == 1)
-                nc.scalar.activation(hs[c][:].rearrange("p (u k m d) -> p k u m d", u=2, k=2, d=2)[:, half],
-                                     pre[:].rearrange("p (m u d) -> p u m d", u=2, d=2),
-                                     mybir.ActivationFunctionType.Gelu_apprx_tanh)
-
-        first_in_halves(0, ((y_pool, "y"), (pre_pool, "pre")))
-        for a in (1, 0):
-            first_pass(1, a, a == 1)
-        activate(1)
-        for a in range(2):
-            gather_words(a, 2, 4, "gw%d_2" % a)
-        for a in range(2):
-            gather_scales(a, 1, "gw%d_0" % a)
-        turn(0)
-        second(0)
-        first_pass(2, 0, True)
-        first_pass(2, 1, False)
-        activate(2)
-        turn(1)
-        second(1)
-        first_in_halves(3, ((pre_pool, "pre"), (tr_pool, "tr")))
-        turn(2)
-        finish(0, S, "h1")
-        row1 = keep.tile([P, S], F32, name="row1", tag="h2", align_bytes=64)
-        nc.vector.tensor_tensor(row1[:], ys[1][:], g[:, S:2 * S], mybir.AluOpType.mult)
-        nc.scalar.activation(res[:].indirect(lists[0][:, LC:2 * LC]), row1[:], mybir.ActivationFunctionType.Copy)
-        second(2)
-        turn(3)
-        row2 = keep.tile([P, S], F32, name="row2", tag="h3", align_bytes=64)
-        nc.vector.tensor_tensor(row2[:], ys[2][:], g[:, 2 * S:3 * S], mybir.AluOpType.mult)
-        second(3)
-        nc.vector.tensor_copy(res[:].indirect(lists[0][:, 2 * LC:3 * LC]), row2[:])
-        finish(3 * S, 4 * S, "h0")
+        rows = {}
+        for c in range(TILES):
+            first(c)
+            second(c)
+            rows[c] = finish(c)
+        nc.vector.tensor_copy(res[:].indirect(lists[0][:, :LC]), rows[0][:])
+        for c in range(1, TILES):
+            nc.vector.tensor_tensor(res[:].indirect(lists[0][:, c * LC:(c + 1) * LC]), rows[c][:], g[:, c * S:(c + 1) * S], mybir.AluOpType.mult)
 
         nc.sync.dma_start(out=out, in_=res[:])

@@ -32,9 +32,7 @@ def tile_moe_duo_gelu_kernel(tc, x_words, x_scales, w1_words, w1_scales, wp_word
         xw = keep.tile([P, T], I32, name="xw", align_bytes=64)
         xs = keep.tile([P, T], U8, name="xs", align_bytes=64)
         lists = [keep.tile([P, E * C // 16], U16, name="list%d" % a) for a in range(2)]
-        raw_wp = keep.tile([P, E, 2 * H], U8, name="raw_wp", align_bytes=64)
-        raw_w1 = [keep.tile([P, 2 * H], U8, name="raw_w1%d" % e, align_bytes=64) for e in range(E)]
-        raw_w = {(1, 0): raw_wp[:, 0, :], (1, 1): raw_wp[:, 1, :], (0, 0): raw_w1[0][:], (0, 1): raw_w1[1][:]}
+        raw_w = {(a, e): keep.tile([P, 2 * H], U8, name="raw_w%d%d" % (a, e), align_bytes=64)[:] for a in range(2) for e in range(E)}
         raw_s = [keep.tile([P, E, H], U8, name="raw_s%d" % a, align_bytes=64) for a in range(2)]
         w2w = keep.tile([P, E, 2 * N], U8, name="w2w", align_bytes=64)
         w2s = keep.tile([P, E, N], U8, name="w2s", align_bytes=64)
@@ -60,20 +58,24 @@ def tile_moe_duo_gelu_kernel(tc, x_words, x_scales, w1_words, w1_scales, wp_word
             rows = scales.rearrange("e s r n -> (e s) r n").bitcast(I32)
             queue.dma_start(out=plane[:].bitcast(I32)[32 * q:32 * q + 4, :, :], in_=rows[:, 4 * q:4 * q + 4, :].rearrange("e r n -> r e n"))
 
-        nc.gpsimd.dma_start(out=raw_wp[:].bitcast(I32), in_=wp_words.rearrange("e s p n -> p (e s) n").bitcast(I32))
-        nc.gpsimd.dma_start(out=raw_w1[1][:].bitcast(I32), in_=w1_words[1, 0].bitcast(I32))
+        def load_words(queue, a, e):
+            queue.dma_start(out=raw_w[a, e].bitcast(I32), in_=(w1_words, wp_words)[a][e, 0].bitcast(I32))
+
+        for a in range(2):
+            load_words(nc.gpsimd, a, 0)
         nc.sync.dma_start(lists[0][:], offs)
         nc.sync.dma_start(lists[1][:], offs2)
         for q in range(4):
             load_token_scales(nc.scalar if q else nc.sync, q)
+        load_quadrant(nc.scalar, raw_s[0], w1_scales, 1)
         nc.sync.dma_start(out=xw[:], in_=x_words[0].rearrange("p n t -> p (n t)").bitcast(I32))
-        nc.scalar.dma_start(out=raw_w1[0][:].bitcast(I32), in_=w1_words[0, 0].bitcast(I32))
         nc.scalar.activation(warm[:, 1:2], warm[:, 0:1], GELU)
+        for q in (0, 2, 3):
+            load_quadrant(nc.sync, raw_s[0], w1_scales, q)
         for q in range(4):
-            load_quadrant(nc.scalar if q % 2 else nc.sync, raw_s[0], w1_scales, q)
-        for q in range(4):
-            load_quadrant(nc.scalar if q == 1 else nc.sync, raw_s[1], wp_scales, q)
-        nc.sync.dma_start(out=w2w[:].bitcast(I32), in_=w2_words.rearrange("e s p n -> p (e s) n").bitcast(I32))
+            load_quadrant(nc.scalar if q % 2 else nc.sync, raw_s[1], wp_scales, q)
+        for a in (1, 0):
+            load_words(nc.sync, a, 1)
         for q in (0, 2):
             load_quadrant(nc.sync, w2s, w2_scales, q)
         nc.sync.dma_start(out=g[:], in_=gate)
@@ -93,6 +95,7 @@ def tile_moe_duo_gelu_kernel(tc, x_words, x_scales, w1_words, w1_scales, wp_word
             if e == 0 and a == 0:
                 for q in (1, 3):
                     load_quadrant(nc.scalar, w2s, w2_scales, q)
+                nc.scalar.dma_start(out=w2w[:].bitcast(I32), in_=w2_words.rearrange("e s p n -> p (e s) n").bitcast(I32))
         for a, e in ((0, 0), (1, 0), (1, 1)):
             deal_scales(a, e, keep.tile([P, H], U8, name="ws%d_%d" % (a, e), align_bytes=64)[:])
         deal_scales(0, 1, raw_s[1][:, 0, :])
@@ -116,8 +119,8 @@ def tile_moe_duo_gelu_kernel(tc, x_words, x_scales, w1_words, w1_scales, wp_word
         gather_words(1, 0, 2)
         gather_words(0, 2, 4)
         gather_words(1, 2, 4)
+        gather_scales(1, 1, "raw_w00")
         gather_scales(0, 1, "raw_w10")
-        gather_scales(1, 1, "raw_wp")
 
         pres, hs, ys = {}, {}, {}
 

@@ -26,7 +26,7 @@ def tile_moe_duo_gelu_kernel(tc, x_words, x_scales, w1_words, w1_scales, wp_word
     with ExitStack() as ctx:
         keep = ctx.enter_context(tc.tile_pool(name="keep", bufs=1))
         work = ctx.enter_context(tc.tile_pool(name="work", bufs=TILES))
-        pre_pool = ctx.enter_context(tc.psum_pool(name="pre", bufs=2))
+        pre_pool = ctx.enter_context(tc.psum_pool(name="pre", bufs=1))
         y_pool = ctx.enter_context(tc.psum_pool(name="y", bufs=4))
 
         xw = keep.tile([P, T], I32, name="xw", align_bytes=64)
@@ -78,16 +78,17 @@ def tile_moe_duo_gelu_kernel(tc, x_words, x_scales, w1_words, w1_scales, wp_word
             load_words(nc.sync, a, 1)
         for q in (0, 2):
             load_quadrant(nc.sync, w2s, w2_scales, q)
-        nc.sync.dma_start(out=g[:], in_=gate)
 
         ww, ws = {}, {}
 
         def deal_words(a, e, to):
-            nc.scalar.copy(to.bitcast(U16).rearrange("p (t m) -> p t m", t=4), raw_w[a, e].bitcast(U16).rearrange("p (m t) -> p t m", t=4))
+            for t in (slice(0, 2), slice(2, 4)) if (a, e) == (1, 0) else (slice(0, 4),):
+                nc.scalar.copy(to.bitcast(U16).rearrange("p (t m) -> p t m", t=4)[:, t, :], raw_w[a, e].bitcast(U16).rearrange("p (m t) -> p t m", t=4)[:, t, :])
             ww[a, e] = to
 
         def deal_scales(a, e, to):
-            nc.gpsimd.tensor_copy(to.rearrange("p (t m) -> p t m", t=4), raw_s[a][:, e, :].rearrange("p (m t) -> p t m", t=4))
+            for t in (slice(0, 2), slice(2, 4)) if (a, e) == (1, 0) else (slice(0, 4),):
+                nc.gpsimd.tensor_copy(to.rearrange("p (t m) -> p t m", t=4)[:, t, :], raw_s[a][:, e, :].rearrange("p (m t) -> p t m", t=4)[:, t, :])
             ws[a, e] = to
 
         for a, e in ((0, 0), (1, 0), (1, 1), (0, 1)):
@@ -96,6 +97,7 @@ def tile_moe_duo_gelu_kernel(tc, x_words, x_scales, w1_words, w1_scales, wp_word
                 for q in (1, 3):
                     load_quadrant(nc.scalar, w2s, w2_scales, q)
                 nc.scalar.dma_start(out=w2w[:].bitcast(I32), in_=w2_words.rearrange("e s p n -> p (e s) n").bitcast(I32))
+                nc.scalar.dma_start(out=g[:], in_=gate)
         for a, e in ((0, 0), (1, 0), (1, 1)):
             deal_scales(a, e, keep.tile([P, H], U8, name="ws%d_%d" % (a, e), align_bytes=64)[:])
         deal_scales(0, 1, raw_s[1][:, 0, :])
@@ -107,8 +109,8 @@ def tile_moe_duo_gelu_kernel(tc, x_words, x_scales, w1_words, w1_scales, wp_word
             nc.vector.tensor_copy(gs[:], xs[:].indirect(lists[a][:, 2 * e * LC:2 * (e + 1) * LC]))
             scales[2 * e, a], scales[2 * e + 1, a] = gs[:, :S], gs[:, S:]
 
-        def gather_words(a, c0, c1):
-            gw = keep.tile([P, (c1 - c0) * S], U32, name="gw%d_%d" % (a, c0), align_bytes=64)
+        def gather_words(a, c0, c1, tag=None):
+            gw = keep.tile([P, (c1 - c0) * S], U32, name="gw%d_%d" % (a, c0), tag=tag or "gw%d_%d" % (a, c0), align_bytes=64)
             nc.vector.tensor_copy(gw[:], xw[:].bitcast(U32).indirect(lists[a][:, c0 * LC:c1 * LC]))
             for c in range(c0, c1):
                 words[c, a] = gw[:, (c - c0) * S:(c - c0 + 1) * S]
@@ -117,8 +119,8 @@ def tile_moe_duo_gelu_kernel(tc, x_words, x_scales, w1_words, w1_scales, wp_word
         gather_scales(1, 0, "gs1")
         gather_words(0, 0, 2)
         gather_words(1, 0, 2)
-        gather_words(0, 2, 4)
         gather_words(1, 2, 4)
+        gather_words(0, 2, 3)
         gather_scales(1, 1, "raw_w00")
         gather_scales(0, 1, "raw_w10")
 
@@ -126,7 +128,7 @@ def tile_moe_duo_gelu_kernel(tc, x_words, x_scales, w1_words, w1_scales, wp_word
 
         def first(c):
             e = c * S // C
-            pre = pre_pool.tile([P, 4, S], F32, name="pre")
+            pre = pre_pool.tile([P, 4, S], F32, name="pre%d" % c, tag="pre%d" % (0 if c == 2 else c))
             order = (1, 0) if c else (0, 1)
             for a in order:
                 for t in range(4):
@@ -134,13 +136,13 @@ def tile_moe_duo_gelu_kernel(tc, x_words, x_scales, w1_words, w1_scales, wp_word
                                         lhsT_scale=ws[a, e][:, t * P:(t + 1) * P],
                                         rhs=words[c, a].bitcast(FP8X4), rhs_scale=scales[c, a],
                                         start=a == order[0] and t == 0, stop=a == order[1] and t == 3)
-            h = work.tile([P, 4 * S], BF16, name="h", align_bytes=64)
+            h = keep.tile([P, 4 * S], BF16, name="h%d" % c, align_bytes=64)
             nc.scalar.activation(h[:].rearrange("p (j t) -> p j t", t=4), pre[:].rearrange("p t j -> p j t"), GELU)
             hs[c] = h
 
         def second(c):
             e = c * S // C
-            hq = work.tile([P, S], U32, name="hq", align_bytes=64)
+            hq = keep.tile([P, S], U32, name="hq%d" % c, tag="hq%d" % max(c - 1, 0), align_bytes=64)
             hscale = work.tile([P, S], U8, name="hscale", align_bytes=64)
             nc.vector.quantize_mx(out=hq[:].bitcast(FP8X4), scales=hscale[:], in_=hs[c][:])
             y = y_pool.tile([P, S], F32, name="y")
@@ -148,21 +150,26 @@ def tile_moe_duo_gelu_kernel(tc, x_words, x_scales, w1_words, w1_scales, wp_word
                                 rhs=hq[:].bitcast(FP8X4), rhs_scale=hscale[:], start=True, stop=True)
             ys[c] = y
 
-        def finish(c):
-            row = work.tile([P, S], F32, name="row", align_bytes=64)
-            if c == 0:
-                nc.vector.tensor_tensor(row[:], ys[c][:], g[:, :S], mybir.AluOpType.mult)
-            else:
-                nc.scalar.copy(row[:], ys[c][:])
-            return row
+        def scatter(row, j0, j1):
+            nc.vector.tensor_tensor(res[:].indirect(lists[0][:, j0 // 16:j1 // 16]), row, g[:, j0:j1], mybir.AluOpType.mult)
 
-        rows = {}
-        for c in range(TILES):
+        first(0)
+        second(0)
+        row0 = keep.tile([P, S], F32, name="row0", align_bytes=64)
+        nc.vector.tensor_tensor(row0[:], ys[0][:], g[:, :S], mybir.AluOpType.mult)
+        gather_words(0, 3, 4, "h0")
+        first(1)
+        second(1)
+        nc.vector.tensor_copy(res[:].indirect(lists[0][:, :LC]), row0[:])
+        for c in (2, 3):
             first(c)
             second(c)
-            rows[c] = finish(c)
-        nc.vector.tensor_copy(res[:].indirect(lists[0][:, :LC]), rows[0][:])
-        for c in range(1, TILES):
-            nc.vector.tensor_tensor(res[:].indirect(lists[0][:, c * LC:(c + 1) * LC]), rows[c][:], g[:, c * S:(c + 1) * S], mybir.AluOpType.mult)
+        row1 = keep.tile([P, S], F32, name="row1", align_bytes=64)
+        nc.scalar.copy(row1[:], ys[1][:])
+        scatter(row1[:], S, 2 * S)
+        row23 = keep.tile([P, 2 * S], F32, name="row23", align_bytes=64)
+        for c in (2, 3):
+            nc.scalar.copy(row23[:, (c - 2) * S:(c - 1) * S], ys[c][:])
+        scatter(row23[:], 2 * S, 4 * S)
 
         nc.sync.dma_start(out=out, in_=res[:])

@@ -130,12 +130,13 @@ def tile_moe_duo_gelu_kernel(tc, x_words, x_scales, w1_words, w1_scales, wp_word
             e = c * S // C
             pre = pre_pool.tile([P, 4, S], F32, name="pre%d" % c, tag="pre%d" % (0 if c == 2 else c))
             order = (1, 0) if c else (0, 1)
+            columns = (3, 2, 1, 0) if c == 1 else (0, 1, 2, 3)
             for a in order:
-                for t in range(4):
+                for t in columns:
                     nc.tensor.matmul_mx(out=pre[:, t, :], lhsT=ww[a, e][:, 2 * t * P:2 * (t + 1) * P].bitcast(FP4X4),
                                         lhsT_scale=ws[a, e][:, t * P:(t + 1) * P],
                                         rhs=words[c, a].bitcast(FP8X4), rhs_scale=scales[c, a],
-                                        start=a == order[0] and t == 0, stop=a == order[1] and t == 3)
+                                        start=a == order[0] and t == columns[0], stop=a == order[1] and t == columns[3])
             h = keep.tile([P, 4 * S], BF16, name="h%d" % c, align_bytes=64)
             nc.scalar.activation(h[:].rearrange("p (j t) -> p j t", t=4), pre[:].rearrange("p t j -> p j t"), GELU)
             hs[c] = h

@@ -87,7 +87,7 @@ def tile_moe_duo_gelu_kernel(tc, x_words, x_scales, w1_words, w1_scales, wp_word
             ww[a, e] = to
 
         def deal_scales(a, e, to):
-            for t in (slice(0, 2), slice(2, 4)) if (a, e) == (1, 0) else (slice(0, 4),):
+            for t in (slice(0, 2), slice(2, 4)) if e == 0 else (slice(0, 4),):
                 nc.gpsimd.tensor_copy(to.rearrange("p (t m) -> p t m", t=4)[:, t, :], raw_s[a][:, e, :].rearrange("p (m t) -> p t m", t=4)[:, t, :])
             ws[a, e] = to
 
@@ -129,14 +129,15 @@ def tile_moe_duo_gelu_kernel(tc, x_words, x_scales, w1_words, w1_scales, wp_word
         def first(c):
             e = c * S // C
             pre = pre_pool.tile([P, 4, S], F32, name="pre%d" % c, tag="pre%d" % (0 if c == 2 else c))
-            order = (1, 0) if c else (0, 1)
-            columns = (3, 2, 1, 0) if c == 1 else (0, 1, 2, 3)
-            for a in order:
-                for t in columns:
-                    nc.tensor.matmul_mx(out=pre[:, t, :], lhsT=ww[a, e][:, 2 * t * P:2 * (t + 1) * P].bitcast(FP4X4),
-                                        lhsT_scale=ws[a, e][:, t * P:(t + 1) * P],
-                                        rhs=words[c, a].bitcast(FP8X4), rhs_scale=scales[c, a],
-                                        start=a == order[0] and t == columns[0], stop=a == order[1] and t == columns[3])
+            if c == 1:
+                passes = [(0, 0), (0, 1)] + [(1, t) for t in (3, 2, 1, 0)] + [(0, 2), (0, 3)]
+            else:
+                passes = [(a, t) for a in ((1, 0) if e else (0, 1)) for t in range(4)]
+            for n, (a, t) in enumerate(passes):
+                nc.tensor.matmul_mx(out=pre[:, t, :], lhsT=ww[a, e][:, 2 * t * P:2 * (t + 1) * P].bitcast(FP4X4),
+                                    lhsT_scale=ws[a, e][:, t * P:(t + 1) * P],
+                                    rhs=words[c, a].bitcast(FP8X4), rhs_scale=scales[c, a],
+                                    start=n == 0, stop=n == len(passes) - 1)
             h = keep.tile([P, 4 * S], BF16, name="h%d" % c, align_bytes=64)
             nc.scalar.activation(h[:].rearrange("p (j t) -> p j t", t=4), pre[:].rearrange("p t j -> p j t"), GELU)
             hs[c] = h

@@ -128,7 +128,7 @@ def tile_moe_duo_gelu_kernel(tc, x_words, x_scales, w1_words, w1_scales, wp_word
 
         def first(c):
             e = c * S // C
-            pre = pre_pool.tile([P, 4, S], F32, name="pre%d" % c, tag="pre%d" % (0 if c == 2 else c))
+            pre = pre_pool.tile([P, 4, S], F32, name="pre%d" % c, tag="pre%d" % c)
             if c == 1:
                 passes = [(0, 0), (0, 1)] + [(1, t) for t in (3, 2, 1, 0)] + [(0, 2), (0, 3)]
             else:
@@ -144,7 +144,7 @@ def tile_moe_duo_gelu_kernel(tc, x_words, x_scales, w1_words, w1_scales, wp_word
 
         def second(c):
             e = c * S // C
-            hq = keep.tile([P, S], U32, name="hq%d" % c, tag="hq%d" % max(c - 1, 0), align_bytes=64)
+            hq = keep.tile([P, S], U32, name="hq%d" % c, tag="hq%d" % (c // 3), align_bytes=64)
             hscale = work.tile([P, S], U8, name="hscale", align_bytes=64)
             nc.vector.quantize_mx(out=hq[:].bitcast(FP8X4), scales=hscale[:], in_=hs[c][:])
             y = y_pool.tile([P, S], F32, name="y")

from contextlib import ExitStack

import concourse.mybir as mybir

K, T, E, C, H, N = 512, 512, 2, 256, 512, 128
FLOPS = 2 * E * C * (2 * K * H + H * N)

F32 = mybir.dt.float32
BF16 = mybir.dt.bfloat16
I32 = mybir.dt.int32
U32 = mybir.dt.uint32
U16 = mybir.dt.uint16
U8 = mybir.dt.uint8
FP8X4 = mybir.dt.float8_e4m3fn_x4
FP4X4 = mybir.dt.float4_e2m1fn_x4
GELU = mybir.ActivationFunctionType.Gelu_apprx_tanh

P = 128
S = 128
TILES = E * C // S
LC = S // 16


def tile_moe_duo_gelu_kernel(tc, x_words, x_scales, w1_words, w1_scales, wp_words, wp_scales, w2_words, w2_scales, gate, offs, offs2, out):
    nc = tc.nc
    with ExitStack() as ctx:
        keep = ctx.enter_context(tc.tile_pool(name="keep", bufs=1))
        work = ctx.enter_context(tc.tile_pool(name="work", bufs=TILES))
        pre_pool = ctx.enter_context(tc.psum_pool(name="pre", bufs=1))
        y_pool = ctx.enter_context(tc.psum_pool(name="y", bufs=4))

        xw = keep.tile([P, T], I32, name="xw", align_bytes=64)
        xs = keep.tile([P, T], U8, name="xs", align_bytes=64)
        lists = [keep.tile([P, E * C // 16], U16, name="list%d" % a) for a in range(2)]
        raw_w = {(a, e): keep.tile([P, 2 * H], U8, name="raw_w%d%d" % (a, e), align_bytes=64)[:] for a in range(2) for e in range(E)}
        raw_s = [keep.tile([P, E, H], U8, name="raw_s%d" % a, align_bytes=64) for a in range(2)]
        w2w = keep.tile([P, E, 2 * N], U8, name="w2w", align_bytes=64)
        w2s = keep.tile([P, E, N], U8, name="w2s", align_bytes=64)
        g = keep.tile([P, E * C], F32, name="g")
        res = keep.tile([P, T], F32, name="res")
        warm = keep.tile([P, 2], F32, name="warm")

        def clear(flat):
            cut = flat.shape[1] // 2 + 1
            nc.vector.memset(flat[:, :cut], 0)
            nc.vector.memset(flat[:, cut:], 0)

        nc.vector.memset(warm[:, 0:1], 0.0)
        clear(raw_s[0][:].rearrange("p e n -> p (e n)").bitcast(I32))
        for plane in (raw_s[1], w2s):
            clear(plane[:].rearrange("p e n -> p (e n)").bitcast(I32))

        def load_token_scales(queue, q):
            rows = x_scales[0, 4 * q:4 * q + 4, :].bitcast(I32)
            queue.dma_start(out=xs[32 * q:32 * q + 32, :].bitcast(I32), in_=rows.unsqueeze(0).broadcast_to([8, 4, T // 4]))

        def load_quadrant(queue, plane, scales, q):
            rows = scales.rearrange("e s r n -> (e s) r n").bitcast(I32)
            queue.dma_start(out=plane[:].bitcast(I32)[32 * q:32 * q + 4, :, :], in_=rows[:, 4 * q:4 * q + 4, :].rearrange("e r n -> r e n"))

        def load_words(queue, a, e):
            queue.dma_start(out=raw_w[a, e].bitcast(I32), in_=(w1_words, wp_words)[a][e, 0].bitcast(I32))

        for a in range(2):
            load_words(nc.gpsimd, a, 0)
        nc.sync.dma_start(lists[0][:], offs)
        nc.sync.dma_start(lists[1][:], offs2)
        for q in range(4):
            load_token_scales(nc.scalar if q else nc.sync, q)
        load_quadrant(nc.scalar, raw_s[0], w1_scales, 1)
        nc.sync.dma_start(out=xw[:], in_=x_words[0].rearrange("p n t -> p (n t)").bitcast(I32))
        nc.scalar.activation(warm[:, 1:2], warm[:, 0:1], GELU)
        for q in (0, 2, 3):
            load_quadrant(nc.sync, raw_s[0], w1_scales, q)
        for q in range(4):
            load_quadrant(nc.scalar if q % 2 else nc.sync, raw_s[1], wp_scales, q)
        for a in (1, 0):
            load_words(nc.sync, a, 1)
        for q in (0, 2):
            load_quadrant(nc.sync, w2s, w2_scales, q)

        ww, ws = {}, {}

        def deal_words(a, e, to):
            for t in (slice(0, 2), slice(2, 4)) if (a, e) == (1, 0) else (slice(0, 4),):
                nc.scalar.copy(to.bitcast(U16).rearrange("p (t m) -> p t m", t=4)[:, t, :], raw_w[a, e].bitcast(U16).rearrange("p (m t) -> p t m", t=4)[:, t, :])
            ww[a, e] = to

        def deal_scales(a, e, to):
            for t in (slice(0, 2), slice(2, 4)) if e == 0 else (slice(0, 4),):
                nc.gpsimd.tensor_copy(to.rearrange("p (t m) -> p t m", t=4)[:, t, :], raw_s[a][:, e, :].rearrange("p (m t) -> p t m", t=4)[:, t, :])
            ws[a, e] = to

        for a, e in ((0, 0), (1, 0), (1, 1), (0, 1)):
            deal_words(a, e, keep.tile([P, 2 * H], U8, name="ww%d_%d" % (a, e), align_bytes=64)[:])
            if e == 0 and a == 0:
                for q in (1, 3):
                    load_quadrant(nc.scalar, w2s, w2_scales, q)
                nc.scalar.dma_start(out=w2w[:].bitcast(I32), in_=w2_words.rearrange("e s p n -> p (e s) n").bitcast(I32))
                nc.scalar.dma_start(out=g[:], in_=gate)
        for a, e in ((0, 0), (1, 0), (1, 1)):
            deal_scales(a, e, keep.tile([P, H], U8, name="ws%d_%d" % (a, e), align_bytes=64)[:])
        deal_scales(0, 1, raw_s[1][:, 0, :])

        words, scales = {}, {}

        def gather_scales(a, e, tag):
            gs = keep.tile([P, C], U8, name="gs%d_%d" % (a, e), tag=tag, align_bytes=64)
            nc.vector.tensor_copy(gs[:], xs[:].indirect(lists[a][:, 2 * e * LC:2 * (e + 1) * LC]))
            scales[2 * e, a], scales[2 * e + 1, a] = gs[:, :S], gs[:, S:]

        def gather_words(a, c0, c1, tag=None):
            gw = keep.tile([P, (c1 - c0) * S], U32, name="gw%d_%d" % (a, c0), tag=tag or "gw%d_%d" % (a, c0), align_bytes=64)
            nc.vector.tensor_copy(gw[:], xw[:].bitcast(U32).indirect(lists[a][:, c0 * LC:c1 * LC]))
            for c in range(c0, c1):
                words[c, a] = gw[:, (c - c0) * S:(c - c0 + 1) * S]

        gather_scales(0, 0, "gs0")
        gather_scales(1, 0, "gs1")
        gather_words(0, 0, 2)
        gather_words(1, 0, 2)
        gather_words(1, 2, 4)
        gather_words(0, 2, 3)
        gather_scales(1, 1, "raw_w00")
        gather_scales(0, 1, "raw_w10")

        pres, hs, ys = {}, {}, {}

        def first(c):
            e = c * S // C
            pre = pre_pool.tile([P, 4, S], F32, name="pre%d" % c, tag="pre%d" % c)
            if c == 1:
                passes = [(0, 0), (0, 1)] + [(1, t) for t in (3, 2, 1, 0)] + [(0, 2), (0, 3)]
            else:
                passes = [(a, t) for a in ((1, 0) if e else (0, 1)) for t in range(4)]
            for n, (a, t) in enumerate(passes):
                nc.tensor.matmul_mx(out=pre[:, t, :], lhsT=ww[a, e][:, 2 * t * P:2 * (t + 1) * P].bitcast(FP4X4),
                                    lhsT_scale=ws[a, e][:, t * P:(t + 1) * P],
                                    rhs=words[c, a].bitcast(FP8X4), rhs_scale=scales[c, a],
                                    start=n == 0, stop=n == len(passes) - 1)
            h = keep.tile([P, 4 * S], BF16, name="h%d" % c, align_bytes=64)
            nc.scalar.activation(h[:].rearrange("p (j t) -> p j t", t=4), pre[:].rearrange("p t j -> p j t"), GELU)
            hs[c] = h

        def second(c):
            e = c * S // C
            hq = keep.tile([P, S], U32, name="hq%d" % c, tag="hq%d" % (c // 3), align_bytes=64)
            hscale = work.tile([P, S], U8, name="hscale", align_bytes=64)
            nc.vector.quantize_mx(out=hq[:].bitcast(FP8X4), scales=hscale[:], in_=hs[c][:])
            y = y_pool.tile([P, S], F32, name="y")
            nc.tensor.matmul_mx(out=y[:], lhsT=w2w[:, e, :].bitcast(FP4X4), lhsT_scale=w2s[:, e, :],
                                rhs=hq[:].bitcast(FP8X4), rhs_scale=hscale[:], start=True, stop=True)
            ys[c] = y

        def scatter(row, j0, j1):
            nc.vector.tensor_tensor(res[:].indirect(lists[0][:, j0 // 16:j1 // 16]), row, g[:, j0:j1], mybir.AluOpType.mult)

        first(0)
        second(0)
        row0 = keep.tile([P, S], F32, name="row0", align_bytes=64)
        nc.vector.tensor_tensor(row0[:], ys[0][:], g[:, :S], mybir.AluOpType.mult)
        gather_words(0, 3, 4, "h0")
        first(1)
        second(1)
        nc.vector.tensor_copy(res[:].indirect(lists[0][:, :LC]), row0[:])
        for c in (2, 3):
            first(c)
            second(c)
        row1 = keep.tile([P, S], F32, name="row1", align_bytes=64)
        nc.scalar.copy(row1[:], ys[1][:])
        scatter(row1[:], S, 2 * S)
        row23 = keep.tile([P, 2 * S], F32, name="row23", align_bytes=64)
        for c in (2, 3):
            nc.scalar.copy(row23[:, (c - 2) * S:(c - 1) * S], ys[c][:])
        scatter(row23[:], 2 * S, 4 * S)

        nc.sync.dma_start(out=out, in_=res[:])
